import numpy as np
import ml_dtypes


def mxq(x, axis, fmt="e4m3"):
    dtype, down = {"e4m3": (ml_dtypes.float8_e4m3fn, 7), "e5m2": (ml_dtypes.float8_e5m2, 14)}[fmt]
    v = np.moveaxis(np.asarray(x, np.float32).astype(ml_dtypes.bfloat16).astype(np.float64), axis, -1)
    blocks = v.reshape(v.shape[:-1] + (-1, 32))
    amax = np.abs(blocks).max(-1, keepdims=True)
    byte = np.maximum(np.where(amax > 0, np.frexp(amax)[1] - 1 + 127, 0) - down, 1)
    scale = np.exp2(byte - 127.0)
    codes = (blocks / scale).astype(np.float32).astype(dtype).astype(np.float64)
    return np.moveaxis((codes * scale).reshape(v.shape), -1, axis)


WIDE = False


def mx_kscale(k):
    if not WIDE:
        return np.ones(k)
    levels = np.array([24, -24, 12, -12, 0])
    if k % 512:
        return np.exp2(np.random.permutation(np.resize(levels, k // 32))).repeat(32)
    a = np.empty((k // 512, 16))
    for p in range(k // 512):
        a[p, :8] = np.random.permutation(np.resize(levels, 8))
        for g in range(8):
            far = levels[np.abs(levels - a[p, g]) >= 10]
            a[p, g + 8] = far[np.random.randint(len(far))]
    return np.exp2(a.ravel()).repeat(32)


def f64(x):
    return np.asarray(x).astype(np.float64)


E2M1 = np.array([0.0, 0.5, 1.0, 1.5, 2.0, 3.0, 4.0, 6.0, -0.0, -0.5, -1.0, -1.5, -2.0, -3.0, -4.0, -6.0])


def pack_weight(w, fmt):
    k, n = w.shape
    w = f64(np.asarray(w, np.float32).astype(ml_dtypes.bfloat16)).reshape(k // 32, 32, n)
    amax = np.abs(w).max(1)
    if fmt == "e4m3":
        byte = np.frexp(amax)[1] - 1 + 127 - 7
    else:
        mant, ex = np.frexp(amax / 6.0)
        byte = np.where(mant > 0.5, ex, ex - 1) + 127
    byte = np.clip(np.where(amax > 0, byte, 1), 1, 254)
    scaled = (w * np.exp2(127.0 - byte)[:, None, :]).reshape(k, n).astype(np.float32)
    by_word = np.ascontiguousarray(scaled.reshape(k // 512, 128, 4, n).transpose(0, 1, 3, 2))
    if fmt == "e4m3":
        words = by_word.astype(ml_dtypes.float8_e4m3fn).view(np.uint8)
    else:
        c = by_word.astype(ml_dtypes.float4_e2m1fn).view(np.uint8) & 0xF
        words = (c[..., 0::2] | (c[..., 1::2] << 4)).reshape(k // 512, 128, 2 * n)
    return np.ascontiguousarray(words), np.ascontiguousarray(byte.astype(np.uint8).reshape(k // 512, 16, n))


def unpack_weight(words, scales, fmt):
    g, _, n = scales.shape
    words = np.ascontiguousarray(words).reshape(g, 128, n, -1)
    if fmt == "e4m3":
        vals = words.view(ml_dtypes.float8_e4m3fn).astype(np.float64)
    else:
        nib = np.empty((g, 128, n, 4), np.uint8)
        nib[..., 0::2] = words & 0xF
        nib[..., 1::2] = words >> 4
        vals = E2M1[nib]
    vals = vals * np.repeat(np.exp2(scales.astype(np.float64) - 127.0), 8, axis=1)[..., None]
    return vals.transpose(0, 1, 3, 2).reshape(g * 512, n)


def planes(y):
    n, m = y.shape
    v = y.astype(np.float32).astype(ml_dtypes.bfloat16).astype(np.float64).reshape(n // 32, 32, m)
    top = np.abs(v).max(1)
    byte = np.clip(np.where(top > 0, np.frexp(top)[1] - 1 + 127 - 7, 1), 1, 254)
    codes = (v * np.exp2(127.0 - byte)[:, None, :]).reshape(n, m).astype(np.float32).astype(ml_dtypes.float8_e4m3fn).view(np.uint8)
    words = codes.reshape(n // 512, 128, 4, m).transpose(0, 1, 3, 2)
    return np.ascontiguousarray(words), np.ascontiguousarray(byte.astype(np.uint8).reshape(n // 512, 16, m))


def gelu(f):
    return 0.5 * f * (1.0 + np.tanh(np.sqrt(2.0 / np.pi) * (f + 0.044715 * f**3)))


K, R, N, T = 512, 1024, 512, 1024


def setup_inputs():
    n = np.random.standard_normal
    u = mx_kscale(R)[:, None]
    s = mx_kscale(K)[:, None]
    p_wu = pack_weight(n((K, R)) / np.sqrt(K) / s * u.T, "e2m1")
    p_v4 = pack_weight(n((R, N)) / np.sqrt(R) / u, "e2m1")
    return {
        "x": (n((K, T)) * s).astype(np.float32),
        "wg": (n((K, R)) / np.sqrt(K) / s).astype(np.float32),
        "wu_words": p_wu[0],
        "wu_scales": p_wu[1],
        "v4_words": p_v4[0],
        "v4_scales": p_v4[1],
        "res": (n((N, T))).astype(np.float32),
    }


def reference(x, wg, wu_words, wu_scales, v4_words, v4_scales, res):
    x_ = mxq(f64(x), 0, "e4m3")
    wg_ = mxq(f64(wg), 0, "e4m3")
    wu_ = unpack_weight(wu_words, wu_scales, "e2m1")
    ga = wg_.T @ x_
    ub = wu_.T @ x_
    h = gelu(ga) * ub
    h_ = mxq(h, 0, "e4m3")
    v4_ = unpack_weight(v4_words, v4_scales, "e2m1")
    y = v4_.T @ h_
    return (f64(res) + y, h) + planes(h)

@@ -1,0 +1,350 @@
+from contextlib import ExitStack
+
+import concourse.mybir as mybir
+
+K, R, N, T = 512, 1024, 512, 1024
+FLOPS = 2 * K * R * T * 2 + 2 * R * N * T
+
+F32 = mybir.dt.float32
+BF16 = mybir.dt.bfloat16
+I32 = mybir.dt.int32
+U32 = mybir.dt.uint32
+U8 = mybir.dt.uint8
+FP8X4 = mybir.dt.float8_e4m3fn_x4
+FP4X4 = mybir.dt.float4_e2m1fn_x4
+ALU = mybir.AluOpType
+GELU = mybir.ActivationFunctionType.Gelu_apprx_tanh
+
+P = 128
+PACK = 4
+PASS = P * PACK
+PASSES = R // PASS
+CHUNK = 256
+CHUNKS = T // CHUNK
+HALF = 512
+Y_COLS = 128
+UNITS = [(0, 0), (1, 0), (0, 1), (1, 1), (2, 0), (2, 1), (3, 0), (3, 1)]
+
+
+def tile_mix_glusave_gelu_res_kernel(
+    tc, x, wg, wu_words, wu_scales, v4_words, v4_scales, res, out_0, out_1, out_2, out_3
+):
+    nc = tc.nc
+    with ExitStack() as ctx:
+        keep = ctx.enter_context(tc.tile_pool(name="keep", bufs=1))
+        stage = ctx.enter_context(tc.tile_pool(name="stage", bufs=3))
+        psum = ctx.enter_context(tc.psum_pool(name="psum", bufs=1))
+        ctx.enter_context(tc.manual_schedule())
+
+        def kept(name, cols, dtype):
+            return keep.tile([P, cols], dtype, name=name, align_bytes=64)
+
+        wu_raw = kept("wu_raw", 2 * R, U8)
+        wu_raw_sc = kept("wu_raw_sc", R, U8)
+        wu_w = kept("wu_w", 2 * R, U8)
+        wu_sc = kept("wu_sc", R, U8)
+        v4_w = kept("v4_w", PASSES * 2 * N, U8)
+        v4_sc = kept("v4_sc", PASSES * N, U8)
+        x_raw = [kept("x_raw%d" % c, PACK * CHUNK, F32) for c in range(CHUNKS)]
+        x_bf = [kept("x_bf%d" % c, PACK * CHUNK, BF16) for c in range(CHUNKS)]
+        x_w = [kept("x_w%d" % c, CHUNK, U32) for c in range(CHUNKS)]
+        x_sc = [kept("x_sc%d" % c, CHUNK, U8) for c in range(CHUNKS)]
+        wg_raw = [[kept("wg_raw%d_%d" % (a, b), PACK * 256, F32) for b in range(2)] for a in range(PASSES)]
+        wg_bf = [kept("wg_bf%d" % a, PACK * PASS, BF16) for a in range(PASSES)]
+        wg_w = [[kept("wg_w%d_%d" % (a, q), 256, U32) for q in range(2)] for a in range(PASSES)]
+        wg_sc = [[kept("wg_sc%d_%d" % (a, q), 256, U8) for q in range(2)] for a in range(PASSES)]
+        res_sb = [kept("res%d" % hf, 4 * HALF, F32) for hf in range(2)]
+        y_sb = [kept("y%d" % hf, 4 * HALF, F32) for hf in range(2)]
+        h_sb = [[kept("h%d_%d" % (hf, a), PACK * HALF, F32) for a in range(PASSES)] for hf in range(2)]
+        h_w = [kept("h_w%d" % hf, PASSES * HALF, U32) for hf in range(2)]
+        h_sc = kept("h_sc", PASSES * T, U8)
+
+        nc.vector.memset(wu_raw_sc[:].bitcast(I32), 0)
+        nc.vector.memset(v4_sc[:].bitcast(I32), 0)
+
+        def load_x(c):
+            nc.sync.dma_start(
+                out=x_raw[c][:].rearrange("p (j t) -> p j t", j=PACK),
+                in_=x[:, c * CHUNK : (c + 1) * CHUNK].rearrange("(p j) t -> p j t", j=PACK),
+            )
+
+        def load_wg(a, b):
+            r0 = a * PASS + b * 256
+            nc.sync.dma_start(
+                out=wg_raw[a][b][:].rearrange("p (j r) -> p j r", j=PACK),
+                in_=wg[:, r0 : r0 + 256].rearrange("(p j) r -> p j r", j=PACK),
+            )
+
+        def load_scales(plane, scales):
+            passes = scales.shape[0]
+            for q in range(4):
+                nc.sync.dma_start(
+                    out=plane[32 * q : 32 * q + 4, :].bitcast(I32).rearrange("p (a n) -> p a n", a=passes),
+                    in_=scales[:, 4 * q : 4 * q + 4, :].rearrange("a r n -> r a n").bitcast(I32),
+                )
+
+        def load_res(hf):
+            nc.sync.dma_start(
+                out=res_sb[hf][:].rearrange("p (i t) -> p i t", i=4),
+                in_=res[:, hf * HALF : (hf + 1) * HALF].rearrange("(i p) t -> p i t", p=P),
+            )
+
+        nc.sync.dma_start(out=wu_raw[:].bitcast(I32), in_=wu_words[0].bitcast(I32))
+        load_x(0)
+        load_scales(wu_raw_sc, wu_scales)
+        load_wg(0, 0)
+        load_wg(0, 1)
+        load_x(1)
+        load_wg(1, 0)
+        load_wg(1, 1)
+        load_x(2)
+        load_scales(v4_sc, v4_scales)
+        nc.sync.dma_start(
+            out=v4_w[:].bitcast(I32).rearrange("p (a n) -> p a n", a=PASSES),
+            in_=v4_words.rearrange("a p n -> p a n").bitcast(I32),
+        )
+        load_x(3)
+        load_res(0)
+        load_res(1)
+
+        def cast(engine, out, in_):
+            if engine == "vector":
+                nc.vector.tensor_copy(out=out, in_=in_)
+            else:
+                nc.scalar.copy(out=out, in_=in_)
+
+        def interleave(engine, dst, src):
+            cast(
+                engine,
+                dst.rearrange("p (c i j) -> p c j i", i=4, j=PACK),
+                src.rearrange("p j (c i) -> p c j i", i=4),
+            )
+
+        def cast_x(engine, c):
+            interleave(engine, x_bf[c][:], x_raw[c][:].rearrange("p (j t) -> p j t", j=PACK))
+
+        def quantize_x(c):
+            nc.vector.quantize_mx(out=x_w[c][:].bitcast(FP8X4), scales=x_sc[c][:], in_=x_bf[c][:])
+
+        def cast_wg(engine, a, b):
+            dst = wg_bf[a][:].rearrange("p (i m j) -> p m i j", i=PACK, j=PACK)
+            cast(
+                engine,
+                dst[:, 64 * b : 64 * (b + 1), :, :],
+                wg_raw[a][b][:].rearrange("p (j m i) -> p m i j", j=PACK, i=PACK),
+            )
+
+        def quantize_wg(a, q):
+            nc.vector.quantize_mx(
+                out=wg_w[a][q][:].bitcast(FP8X4),
+                scales=wg_sc[a][q][:],
+                in_=wg_bf[a][:, q * 1024 : (q + 1) * 1024],
+            )
+
+        gate_banks = {}
+        up_banks = {}
+        gelus = {}
+        h_bf = {}
+        y_banks = {}
+
+        def gate_matmuls(u, q):
+            c, a = UNITS[u]
+            bank = psum.tile([P, 2 * CHUNK], F32, name="gate", bufs=3)
+            for e in range(2):
+                nc.tensor.matmul_mx(
+                    out=bank[:, e * CHUNK : (e + 1) * CHUNK],
+                    lhsT=wg_w[a][q][:, e * P : (e + 1) * P].bitcast(FP8X4),
+                    lhsT_scale=wg_sc[a][q][:, e * P : (e + 1) * P],
+                    rhs=x_w[c][:].bitcast(FP8X4),
+                    rhs_scale=x_sc[c][:],
+                    start=True,
+                    stop=True,
+                )
+            gate_banks[(u, q)] = bank
+
+        def up_matmuls(u, q):
+            c, a = UNITS[u]
+            bank = psum.tile([P, 2 * CHUNK], F32, name="up", bufs=3)
+            for e in range(2):
+                m0 = a * PASS + (2 * q + e) * P
+                nc.tensor.matmul_mx(
+                    out=bank[:, e * CHUNK : (e + 1) * CHUNK],
+                    lhsT=wu_w[:, 2 * m0 : 2 * (m0 + P)].bitcast(FP4X4),
+                    lhsT_scale=wu_sc[:, m0 : m0 + P],
+                    rhs=x_w[c][:].bitcast(FP8X4),
+                    rhs_scale=x_sc[c][:],
+                    start=True,
+                    stop=True,
+                )
+            up_banks[(u, q)] = bank
+
+        def gelu(u, q):
+            act = stage.tile([P, 2 * CHUNK], F32, name="act")
+            nc.scalar.activation(out=act[:], in_=gate_banks[(u, q)][:], func=GELU)
+            gelus[(u, q)] = act
+
+        def h_view(c, a):
+            t0 = (c % 2) * CHUNK
+            return h_sb[c // 2][a][:].rearrange("p (i t) -> p i t", i=PACK)[:, :, t0 : t0 + CHUNK]
+
+        def multiply(u, q):
+            c, a = UNITS[u]
+            nc.vector.tensor_tensor(
+                out=h_view(c, a)[:, 2 * q : 2 * q + 2, :],
+                in0=up_banks[(u, q)][:].rearrange("p (e t) -> p e t", e=2),
+                in1=gelus[(u, q)][:].rearrange("p (e t) -> p e t", e=2),
+                op=ALU.mult,
+            )
+
+        def cast_h(u):
+            c, a = UNITS[u]
+            rounded = stage.tile([P, PACK * CHUNK], BF16, name="rounded", align_bytes=64)
+            interleave("scalar", rounded[:], h_view(c, a))
+            h_bf[u] = rounded
+
+        def h_words(c, a, t0, width):
+            w0 = a * HALF + (c % 2) * CHUNK + t0
+            return h_w[c // 2][:, w0 : w0 + width]
+
+        def h_scales(c, a, t0, width):
+            s0 = a * T + c * CHUNK + t0
+            return h_sc[:, s0 : s0 + width]
+
+        def quantize_h(u):
+            c, a = UNITS[u]
+            nc.vector.quantize_mx(
+                out=h_words(c, a, 0, CHUNK).bitcast(FP8X4), scales=h_scales(c, a, 0, CHUNK), in_=h_bf[u][:]
+            )
+
+        def down_matmuls(c, q):
+            bank = psum.tile([P, 2 * CHUNK], F32, name="down", bufs=2)
+            for e in range(2):
+                n0 = (2 * q + e) * P
+                for t0 in range(0, CHUNK, Y_COLS):
+                    for a in range(PASSES):
+                        nc.tensor.matmul_mx(
+                            out=bank[:, e * CHUNK + t0 : e * CHUNK + t0 + Y_COLS],
+                            lhsT=v4_w[:, 2 * (a * N + n0) : 2 * (a * N + n0 + P)].bitcast(FP4X4),
+                            lhsT_scale=v4_sc[:, a * N + n0 : a * N + n0 + P],
+                            rhs=h_words(c, a, t0, Y_COLS).bitcast(FP8X4),
+                            rhs_scale=h_scales(c, a, t0, Y_COLS),
+                            start=(a == 0),
+                            stop=(a == PASSES - 1),
+                        )
+            y_banks[(c, q)] = bank
+
+        def n_view(tiles, c):
+            t0 = (c % 2) * CHUNK
+            return tiles[c // 2][:].rearrange("p (i t) -> p i t", i=4)[:, :, t0 : t0 + CHUNK]
+
+        def add_res(c, q):
+            nc.vector.tensor_tensor(
+                out=n_view(y_sb, c)[:, 2 * q : 2 * q + 2, :],
+                in0=y_banks[(c, q)][:].rearrange("p (e t) -> p e t", e=2),
+                in1=n_view(res_sb, c)[:, 2 * q : 2 * q + 2, :],
+                op=ALU.add,
+            )
+
+        def store_h(a, c0, c1):
+            t0 = (c0 % 2) * CHUNK
+            src = h_sb[c0 // 2][a][:].rearrange("p (i t) -> p i t", i=PACK)
+            nc.sync.dma_start(
+                out=out_1[a * PASS : (a + 1) * PASS, c0 * CHUNK : c1 * CHUNK].rearrange("(p i) t -> p i t", i=PACK),
+                in_=src[:, :, t0 : t0 + (c1 - c0) * CHUNK],
+            )
+
+        def store_words(c0, c1):
+            t0 = (c0 % 2) * CHUNK
+            src = h_w[c0 // 2][:].bitcast(I32).rearrange("p (a t) -> p a t", a=PASSES)
+            nc.sync.dma_start(
+                out=out_2[:, :, c0 * CHUNK : c1 * CHUNK, :].rearrange("a p t i -> p a (t i)").bitcast(I32),
+                in_=src[:, :, t0 : t0 + (c1 - c0) * CHUNK],
+            )
+
+        def store_scales():
+            for q in range(4):
+                nc.scalar.dma_start(
+                    out=out_3[:, 4 * q : 4 * q + 4, :].rearrange("a r t -> r a t").bitcast(I32),
+                    in_=h_sc[32 * q : 32 * q + 4, :].bitcast(I32).rearrange("p (a t) -> p a t", a=PASSES),
+                )
+
+        def store_y(c0, c1, i0, i1):
+            t0 = (c0 % 2) * CHUNK
+            src = y_sb[c0 // 2][:].rearrange("p (i t) -> p i t", i=4)
+            nc.sync.dma_start(
+                out=out_0[i0 * P : i1 * P, c0 * CHUNK : c1 * CHUNK].rearrange("(i p) t -> p i t", p=P),
+                in_=src[:, i0:i1, t0 : t0 + (c1 - c0) * CHUNK],
+            )
+
+        nc.vector.tensor_copy(
+            out=wu_w[:].rearrange("p (a i m b) -> p a i m b", a=PASSES, i=PACK, b=2),
+            in_=wu_raw[:].rearrange("p (a m i b) -> p a i m b", a=PASSES, i=PACK, b=2),
+        )
+        cast_x("scalar", 0)
+        nc.vector.tensor_copy(
+            out=wu_sc[:].rearrange("p (a i m) -> p a i m", a=PASSES, i=PACK),
+            in_=wu_raw_sc[:].rearrange("p (a m i) -> p a i m", a=PASSES, i=PACK),
+        )
+        cast_wg("vector", 0, 0)
+        quantize_x(0)
+        up_matmuls(0, 0)
+        up_matmuls(0, 1)
+        cast_wg("vector", 0, 1)
+        for q in range(2):
+            quantize_wg(0, q)
+            gate_matmuls(0, q)
+        cast_x("vector", 1)
+
+        last = len(UNITS) - 1
+        pending = None
+        for f in range(last + 3):
+            if f == 1:
+                quantize_wg(1, 0)
+                quantize_wg(1, 1)
+            if f in (3, 4):
+                quantize_x(f - 1)
+            if f <= last:
+                gelu(f, 0)
+                multiply(f, 0)
+            if f == 0:
+                cast_wg("scalar", 1, 0)
+                quantize_x(1)
+            if 1 <= f <= last + 1:
+                cast_h(f - 1)
+            if f + 1 <= last:
+                for q in range(2):
+                    gate_matmuls(f + 1, q)
+                    up_matmuls(f + 1, q)
+            adding = pending
+            pending = None
+            if adding is not None:
+                down_matmuls(adding, 1)
+                add_res(adding, 0)
+                if adding == CHUNKS - 1:
+                    store_y(adding, adding + 1, 0, 2)
+            if f == 0:
+                cast_wg("vector", 1, 1)
+            if f in (2, 3):
+                cast_x("vector", f)
+            if 1 <= f <= last + 1:
+                quantize_h(f - 1)
+                c, a = UNITS[f - 1]
+                if a == PASSES - 1:
+                    pending = c
+                    down_matmuls(c, 0)
+                    if c >= 1:
+                        store_words(0 if c == 1 else c, c + 1)
+                    if c == CHUNKS - 1:
+                        store_scales()
+            if f <= last:
+                gelu(f, 1)
+                multiply(f, 1)
+                c, a = UNITS[f]
+                if c >= 1:
+                    store_h(a, 0 if c == 1 else c, c + 1)
+            if adding is not None:
+                add_res(adding, 1)
+                if adding == CHUNKS - 1:
+                    store_y(adding, adding + 1, 2, 4)
+                elif adding >= 1:
+                    store_y(0 if adding == 1 else adding, adding + 1, 0, 4)

@@ -23,7 +23,12 @@ CHUNK = 256
 CHUNKS = T // CHUNK
 HALF = 512
 Y_COLS = 128
-UNITS = [(0, 0), (1, 0), (0, 1), (1, 1), (2, 0), (2, 1), (3, 0), (3, 1)]
+UNITS = [(0, 256, 0), (256, 256, 0), (0, 256, 1), (256, 256, 1), (512, 256, 0), (512, 256, 1), (768, 256, 0), (768, 128, 1), (896, 128, 1)]
+BANK = 512
+LAG = 2
+ADD_LAG = 2
+EARLY_FROM = 768
+VCAST_FROM = 9
 
 
 def tile_mix_glusave_gelu_res_kernel(
@@ -45,7 +50,8 @@ def tile_mix_glusave_gelu_res_kernel(
         wu_sc = kept("wu_sc", R, U8)
         v4_w = kept("v4_w", PASSES * 2 * N, U8)
         v4_sc = kept("v4_sc", PASSES * N, U8)
-        x_raw = [kept("x_raw%d" % c, PACK * CHUNK, F32) for c in range(CHUNKS)]
+        x_loads = [(0, 1), (1, 1), (2, 2)]
+        x_raw = [kept("x_raw%d" % c, PACK * n * CHUNK, F32) for c, n in x_loads]
         x_bf = [kept("x_bf%d" % c, PACK * CHUNK, BF16) for c in range(CHUNKS)]
         x_w = [kept("x_w%d" % c, CHUNK, U32) for c in range(CHUNKS)]
         x_sc = [kept("x_sc%d" % c, CHUNK, U8) for c in range(CHUNKS)]
@@ -53,7 +59,7 @@ def tile_mix_glusave_gelu_res_kernel(
         wg_bf = [kept("wg_bf%d" % a, PACK * PASS, BF16) for a in range(PASSES)]
         wg_w = [[kept("wg_w%d_%d" % (a, q), 256, U32) for q in range(2)] for a in range(PASSES)]
         wg_sc = [[kept("wg_sc%d_%d" % (a, q), 256, U8) for q in range(2)] for a in range(PASSES)]
-        res_sb = [kept("res%d" % hf, 4 * HALF, F32) for hf in range(2)]
+        res_sb = kept("res", 4 * T, F32)
         y_sb = [kept("y%d" % hf, 4 * HALF, F32) for hf in range(2)]
         h_sb = [[kept("h%d_%d" % (hf, a), PACK * HALF, F32) for a in range(PASSES)] for hf in range(2)]
         h_w = [kept("h_w%d" % hf, PASSES * HALF, U32) for hf in range(2)]
@@ -62,10 +68,11 @@ def tile_mix_glusave_gelu_res_kernel(
         nc.vector.memset(wu_raw_sc[:].bitcast(I32), 0)
         nc.vector.memset(v4_sc[:].bitcast(I32), 0)
 
-        def load_x(c):
+        def load_x(g):
+            c, n = x_loads[g]
             nc.sync.dma_start(
-                out=x_raw[c][:].rearrange("p (j t) -> p j t", j=PACK),
-                in_=x[:, c * CHUNK : (c + 1) * CHUNK].rearrange("(p j) t -> p j t", j=PACK),
+                out=x_raw[g][:].rearrange("p (j t) -> p j t", j=PACK),
+                in_=x[:, c * CHUNK : (c + n) * CHUNK].rearrange("(p j) t -> p j t", j=PACK),
             )
 
         def load_wg(a, b):
@@ -85,8 +92,8 @@ def tile_mix_glusave_gelu_res_kernel(
 
         def load_res(hf):
             nc.sync.dma_start(
-                out=res_sb[hf][:].rearrange("p (i t) -> p i t", i=4),
-                in_=res[:, hf * HALF : (hf + 1) * HALF].rearrange("(i p) t -> p i t", p=P),
+                out=res_sb[:].rearrange("p (i t) -> p i t", i=4),
+                in_=res.rearrange("(i p) t -> p i t", p=P),
             )
 
         nc.sync.dma_start(out=wu_raw[:].bitcast(I32), in_=wu_words[0].bitcast(I32))
@@ -103,9 +110,7 @@ def tile_mix_glusave_gelu_res_kernel(
             out=v4_w[:].bitcast(I32).rearrange("p (a n) -> p a n", a=PASSES),
             in_=v4_words.rearrange("a p n -> p a n").bitcast(I32),
         )
-        load_x(3)
         load_res(0)
-        load_res(1)
 
         def cast(engine, out, in_):
             if engine == "vector":
@@ -121,7 +126,7 @@ def tile_mix_glusave_gelu_res_kernel(
             )
 
         def cast_x(engine, c):
-            interleave(engine, x_bf[c][:], x_raw[c][:].rearrange("p (j t) -> p j t", j=PACK))
+            interleave(engine, x_bf[c][:], x_raw[min(c, 2)][:].rearrange("p (j t) -> p j t", j=PACK)[:, :, max(c - 2, 0) * CHUNK : (max(c - 2, 0) + 1) * CHUNK])
 
         def quantize_x(c):
             nc.vector.quantize_mx(out=x_w[c][:].bitcast(FP8X4), scales=x_sc[c][:], in_=x_bf[c][:])
@@ -141,139 +146,145 @@ def tile_mix_glusave_gelu_res_kernel(
                 in_=wg_bf[a][:, q * 1024 : (q + 1) * 1024],
             )
 
+        steps = []
+        last_step = []
+        for u, (t0, width, a) in enumerate(UNITS):
+            per_bank = BANK // width
+            steps.extend((u, i0, per_bank) for i0 in range(0, PACK, per_bank))
+            last_step.append(len(steps) - 1)
+
         gate_banks = {}
         up_banks = {}
         gelus = {}
         h_bf = {}
         y_banks = {}
 
-        def gate_matmuls(u, q):
-            c, a = UNITS[u]
-            bank = psum.tile([P, 2 * CHUNK], F32, name="gate", bufs=3)
-            for e in range(2):
+        def x_operand(t0, width):
+            c, w0 = divmod(t0, CHUNK)
+            return x_w[c][:, w0 : w0 + width].bitcast(FP8X4), x_sc[c][:, w0 : w0 + width]
+
+        def gate_matmuls(s):
+            u, i0, count = steps[s]
+            t0, width, a = UNITS[u]
+            rhs, rhs_scale = x_operand(t0, width)
+            bank = psum.tile([P, BANK], F32, name="gate", bufs=3)
+            for e in range(count):
+                q, m0 = divmod((i0 + e) * P, 256)
                 nc.tensor.matmul_mx(
-                    out=bank[:, e * CHUNK : (e + 1) * CHUNK],
-                    lhsT=wg_w[a][q][:, e * P : (e + 1) * P].bitcast(FP8X4),
-                    lhsT_scale=wg_sc[a][q][:, e * P : (e + 1) * P],
-                    rhs=x_w[c][:].bitcast(FP8X4),
-                    rhs_scale=x_sc[c][:],
+                    out=bank[:, e * width : (e + 1) * width],
+                    lhsT=wg_w[a][q][:, m0 : m0 + P].bitcast(FP8X4),
+                    lhsT_scale=wg_sc[a][q][:, m0 : m0 + P],
+                    rhs=rhs,
+                    rhs_scale=rhs_scale,
                     start=True,
                     stop=True,
                 )
-            gate_banks[(u, q)] = bank
+            gate_banks[s] = bank
 
-        def up_matmuls(u, q):
-            c, a = UNITS[u]
-            bank = psum.tile([P, 2 * CHUNK], F32, name="up", bufs=3)
-            for e in range(2):
-                m0 = a * PASS + (2 * q + e) * P
+        def up_matmuls(s):
+            u, i0, count = steps[s]
+            t0, width, a = UNITS[u]
+            rhs, rhs_scale = x_operand(t0, width)
+            bank = psum.tile([P, BANK], F32, name="up", bufs=3)
+            for e in range(count):
+                m0 = a * PASS + (i0 + e) * P
                 nc.tensor.matmul_mx(
-                    out=bank[:, e * CHUNK : (e + 1) * CHUNK],
+                    out=bank[:, e * width : (e + 1) * width],
                     lhsT=wu_w[:, 2 * m0 : 2 * (m0 + P)].bitcast(FP4X4),
                     lhsT_scale=wu_sc[:, m0 : m0 + P],
-                    rhs=x_w[c][:].bitcast(FP8X4),
-                    rhs_scale=x_sc[c][:],
+                    rhs=rhs,
+                    rhs_scale=rhs_scale,
                     start=True,
                     stop=True,
                 )
-            up_banks[(u, q)] = bank
+            up_banks[s] = bank
 
-        def gelu(u, q):
-            act = stage.tile([P, 2 * CHUNK], F32, name="act")
-            nc.scalar.activation(out=act[:], in_=gate_banks[(u, q)][:], func=GELU)
-            gelus[(u, q)] = act
+        def gelu(s):
+            act = stage.tile([P, BANK], F32, name="act", bufs=4)
+            nc.scalar.activation(out=act[:], in_=gate_banks[s][:], func=GELU)
+            gelus[s] = act
 
-        def h_view(c, a):
-            t0 = (c % 2) * CHUNK
-            return h_sb[c // 2][a][:].rearrange("p (i t) -> p i t", i=PACK)[:, :, t0 : t0 + CHUNK]
+        def rows_view(tile, t0, width):
+            w0 = t0 % HALF
+            return tile[:].rearrange("p (i t) -> p i t", i=4)[:, :, w0 : w0 + width]
 
-        def multiply(u, q):
-            c, a = UNITS[u]
+        def multiply(s):
+            u, i0, count = steps[s]
+            t0, width, a = UNITS[u]
             nc.vector.tensor_tensor(
-                out=h_view(c, a)[:, 2 * q : 2 * q + 2, :],
-                in0=up_banks[(u, q)][:].rearrange("p (e t) -> p e t", e=2),
-                in1=gelus[(u, q)][:].rearrange("p (e t) -> p e t", e=2),
+                out=rows_view(h_sb[t0 // HALF][a], t0, width)[:, i0 : i0 + count, :],
+                in0=up_banks[s][:].rearrange("p (e t) -> p e t", e=count),
+                in1=gelus[s][:].rearrange("p (e t) -> p e t", e=count),
                 op=ALU.mult,
             )
 
-        def cast_h(u):
-            c, a = UNITS[u]
-            rounded = stage.tile([P, PACK * CHUNK], BF16, name="rounded", align_bytes=64)
-            interleave("scalar", rounded[:], h_view(c, a))
+        def cast_h(engine, u):
+            t0, width, a = UNITS[u]
+            rounded = stage.tile([P, PACK * width], BF16, name="rounded", align_bytes=64)
+            interleave(engine, rounded[:], rows_view(h_sb[t0 // HALF][a], t0, width))
             h_bf[u] = rounded
 
-        def h_words(c, a, t0, width):
-            w0 = a * HALF + (c % 2) * CHUNK + t0
-            return h_w[c // 2][:, w0 : w0 + width]
+        def h_words(a, t0, width):
+            w0 = a * HALF + t0 % HALF
+            return h_w[t0 // HALF][:, w0 : w0 + width]
 
-        def h_scales(c, a, t0, width):
-            s0 = a * T + c * CHUNK + t0
-            return h_sc[:, s0 : s0 + width]
+        def h_scales(a, t0, width):
+            return h_sc[:, a * T + t0 : a * T + t0 + width]
 
         def quantize_h(u):
-            c, a = UNITS[u]
+            t0, width, a = UNITS[u]
             nc.vector.quantize_mx(
-                out=h_words(c, a, 0, CHUNK).bitcast(FP8X4), scales=h_scales(c, a, 0, CHUNK), in_=h_bf[u][:]
+                out=h_words(a, t0, width).bitcast(FP8X4), scales=h_scales(a, t0, width), in_=h_bf[u][:]
             )
 
-        def down_matmuls(c, q):
-            bank = psum.tile([P, 2 * CHUNK], F32, name="down", bufs=2)
-            for e in range(2):
-                n0 = (2 * q + e) * P
-                for t0 in range(0, CHUNK, Y_COLS):
-                    for a in range(PASSES):
-                        nc.tensor.matmul_mx(
-                            out=bank[:, e * CHUNK + t0 : e * CHUNK + t0 + Y_COLS],
-                            lhsT=v4_w[:, 2 * (a * N + n0) : 2 * (a * N + n0 + P)].bitcast(FP4X4),
-                            lhsT_scale=v4_sc[:, a * N + n0 : a * N + n0 + P],
-                            rhs=h_words(c, a, t0, Y_COLS).bitcast(FP8X4),
-                            rhs_scale=h_scales(c, a, t0, Y_COLS),
-                            start=(a == 0),
-                            stop=(a == PASSES - 1),
-                        )
-            y_banks[(c, q)] = bank
+        def down_pass(t0, a):
+            if a == 0:
+                y_banks[t0] = psum.tile([P, BANK], F32, name="down", bufs=2)
+            for i in range(4):
+                n0 = a * N + i * P
+                nc.tensor.matmul_mx(
+                    out=y_banks[t0][:, i * Y_COLS : (i + 1) * Y_COLS],
+                    lhsT=v4_w[:, 2 * n0 : 2 * (n0 + P)].bitcast(FP4X4),
+                    lhsT_scale=v4_sc[:, n0 : n0 + P],
+                    rhs=h_words(a, t0, Y_COLS).bitcast(FP8X4),
+                    rhs_scale=h_scales(a, t0, Y_COLS),
+                    start=(a == 0 and i == 0),
+                    stop=(a == PASSES - 1 and i == 3),
+                )
 
-        def n_view(tiles, c):
-            t0 = (c % 2) * CHUNK
-            return tiles[c // 2][:].rearrange("p (i t) -> p i t", i=4)[:, :, t0 : t0 + CHUNK]
-
-        def add_res(c, q):
+        def add_res(t0):
             nc.vector.tensor_tensor(
-                out=n_view(y_sb, c)[:, 2 * q : 2 * q + 2, :],
-                in0=y_banks[(c, q)][:].rearrange("p (e t) -> p e t", e=2),
-                in1=n_view(res_sb, c)[:, 2 * q : 2 * q + 2, :],
+                out=rows_view(y_sb[t0 // HALF], t0, Y_COLS),
+                in0=y_banks[t0][:].rearrange("p (i t) -> p i t", i=4),
+                in1=res_sb[:].rearrange("p (i t) -> p i t", i=4)[:, :, t0 : t0 + Y_COLS],
                 op=ALU.add,
             )
 
-        def store_h(a, c0, c1):
-            t0 = (c0 % 2) * CHUNK
-            src = h_sb[c0 // 2][a][:].rearrange("p (i t) -> p i t", i=PACK)
+        def store_h(a, t0, t1):
             nc.sync.dma_start(
-                out=out_1[a * PASS : (a + 1) * PASS, c0 * CHUNK : c1 * CHUNK].rearrange("(p i) t -> p i t", i=PACK),
-                in_=src[:, :, t0 : t0 + (c1 - c0) * CHUNK],
+                out=out_1[a * PASS : (a + 1) * PASS, t0:t1].rearrange("(p i) t -> p i t", i=PACK),
+                in_=rows_view(h_sb[t0 // HALF][a], t0, t1 - t0),
             )
 
-        def store_words(c0, c1):
-            t0 = (c0 % 2) * CHUNK
-            src = h_w[c0 // 2][:].bitcast(I32).rearrange("p (a t) -> p a t", a=PASSES)
+        def store_words(t0, t1):
+            w0 = t0 % HALF
+            src = h_w[t0 // HALF][:].bitcast(I32).rearrange("p (a t) -> p a t", a=PASSES)
             nc.sync.dma_start(
-                out=out_2[:, :, c0 * CHUNK : c1 * CHUNK, :].rearrange("a p t i -> p a (t i)").bitcast(I32),
-                in_=src[:, :, t0 : t0 + (c1 - c0) * CHUNK],
+                out=out_2[:, :, t0:t1, :].rearrange("a p t i -> p a (t i)").bitcast(I32),
+                in_=src[:, :, w0 : w0 + t1 - t0],
             )
 
         def store_scales():
             for q in range(4):
-                nc.scalar.dma_start(
+                nc.sync.dma_start(
                     out=out_3[:, 4 * q : 4 * q + 4, :].rearrange("a r t -> r a t").bitcast(I32),
                     in_=h_sc[32 * q : 32 * q + 4, :].bitcast(I32).rearrange("p (a t) -> p a t", a=PASSES),
                 )
 
-        def store_y(c0, c1, i0, i1):
-            t0 = (c0 % 2) * CHUNK
-            src = y_sb[c0 // 2][:].rearrange("p (i t) -> p i t", i=4)
+        def store_y(t0, t1):
             nc.sync.dma_start(
-                out=out_0[i0 * P : i1 * P, c0 * CHUNK : c1 * CHUNK].rearrange("(i p) t -> p i t", p=P),
-                in_=src[:, i0:i1, t0 : t0 + (c1 - c0) * CHUNK],
+                out=out_0[:, t0:t1].rearrange("(i p) t -> p i t", p=P),
+                in_=rows_view(y_sb[t0 // HALF], t0, t1 - t0),
             )
 
         nc.vector.tensor_copy(
@@ -285,66 +296,86 @@ def tile_mix_glusave_gelu_res_kernel(
             out=wu_sc[:].rearrange("p (a i m) -> p a i m", a=PASSES, i=PACK),
             in_=wu_raw_sc[:].rearrange("p (a m i) -> p a i m", a=PASSES, i=PACK),
         )
-        cast_wg("vector", 0, 0)
         quantize_x(0)
-        up_matmuls(0, 0)
-        up_matmuls(0, 1)
+        up_matmuls(0)
+        up_matmuls(1)
+        cast_wg("vector", 0, 0)
         cast_wg("vector", 0, 1)
-        for q in range(2):
-            quantize_wg(0, q)
-            gate_matmuls(0, q)
+        for s in range(2):
+            quantize_wg(0, s)
+            gate_matmuls(s)
         cast_x("vector", 1)
+        quantize_x(1)
+        gate_matmuls(2)
+        up_matmuls(2)
 
-        last = len(UNITS) - 1
-        pending = None
-        for f in range(last + 3):
-            if f == 1:
-                quantize_wg(1, 0)
-                quantize_wg(1, 1)
-            if f in (3, 4):
-                quantize_x(f - 1)
-            if f <= last:
-                gelu(f, 0)
-                multiply(f, 0)
-            if f == 0:
-                cast_wg("scalar", 1, 0)
-                quantize_x(1)
-            if 1 <= f <= last + 1:
-                cast_h(f - 1)
-            if f + 1 <= last:
-                for q in range(2):
-                    gate_matmuls(f + 1, q)
-                    up_matmuls(f + 1, q)
-            adding = pending
-            pending = None
-            if adding is not None:
-                down_matmuls(adding, 1)
-                add_res(adding, 0)
-                if adding == CHUNKS - 1:
-                    store_y(adding, adding + 1, 0, 2)
-            if f == 0:
-                cast_wg("vector", 1, 1)
-            if f in (2, 3):
-                cast_x("vector", f)
-            if 1 <= f <= last + 1:
-                quantize_h(f - 1)
-                c, a = UNITS[f - 1]
-                if a == PASSES - 1:
-                    pending = c
-                    down_matmuls(c, 0)
-                    if c >= 1:
-                        store_words(0 if c == 1 else c, c + 1)
-                    if c == CHUNKS - 1:
-                        store_scales()
-            if f <= last:
-                gelu(f, 1)
-                multiply(f, 1)
-                c, a = UNITS[f]
-                if c >= 1:
-                    store_h(a, 0 if c == 1 else c, c + 1)
-            if adding is not None:
-                add_res(adding, 1)
-                if adding == CHUNKS - 1:
-                    store_y(adding, adding + 1, 2, 4)
-                elif adding >= 1:
-                    store_y(0 if adding == 1 else adding, adding + 1, 0, 4)
+        H_STORES = [{512: 0, 768: 512, 1024: 768}, {256: 0, 512: 256, 768: 512, 1024: 768}]
+        W_STORES = {256: 0, 512: 256, 768: 512, 1024: 768}
+        Y_STORES = {256: 0, 512: 256, 768: 512, 896: 768, 1024: 896}
+        before = {0: [lambda: cast_wg("vector", 1, 0)]}
+        after = {
+            0: [lambda: cast_wg("vector", 1, 1)],
+            1: [lambda: quantize_wg(1, 0), lambda: quantize_wg(1, 1)],
+            2: [lambda: cast_x("vector", 2)],
+            3: [lambda: quantize_x(2)], 4: [lambda: cast_x("vector", 3)],
+            5: [lambda: quantize_x(3)],
+        }
+        waiting = []
+        summed = []
+        opened = list(range(0, T, Y_COLS))
+        quantized = set()
+        started = []
+
+        def advance_down(s):
+            for t0 in list(started):
+                if (1, t0) in quantized:
+                    down_pass(t0, 1)
+                    started.remove(t0)
+                    summed.append((t0, s))
+            while opened and len(started) + len(summed) < 2 and (0, opened[0]) in quantized and (
+                (1, opened[0]) in quantized or opened[0] >= EARLY_FROM
+            ):
+                t0 = opened.pop(0)
+                down_pass(t0, 0)
+                if (1, t0) in quantized:
+                    down_pass(t0, 1)
+                    summed.append((t0, s))
+                else:
+                    started.append(t0)
+
+        for s in range(len(steps) + 6):
+            if s < len(steps):
+                gelu(s)
+            done = [u for u in range(len(UNITS)) if last_step[u] + LAG == s]
+            for u in done:
+                if u < VCAST_FROM:
+                    cast_h("scalar", u)
+            for job in before.get(s, []):
+                job()
+            if s < len(steps):
+                multiply(s)
+                t0, width, a = UNITS[steps[s][0]]
+                if s in last_step and t0 + width in H_STORES[a]:
+                    store_h(a, H_STORES[a][t0 + width], t0 + width)
+            for job in after.get(s, []):
+                job()
+            if s + 3 < len(steps):
+                gate_matmuls(s + 3)
+                up_matmuls(s + 3)
+            if summed and summed[0][1] + ADD_LAG <= s:
+                t0 = summed.pop(0)[0]
+                add_res(t0)
+                if t0 + Y_COLS in Y_STORES:
+                    store_y(Y_STORES[t0 + Y_COLS], t0 + Y_COLS)
+            for u in range(VCAST_FROM, len(UNITS)):
+                if last_step[u] + 1 == s:
+                    cast_h("vector", u)
+            for u in done:
+                quantize_h(u)
+                t0, width, a = UNITS[u]
+                for t in range(t0, t0 + width, Y_COLS):
+                    quantized.add((a, t))
+                if a == PASSES - 1 and t0 + width in W_STORES:
+                    store_words(W_STORES[t0 + width], t0 + width)
+            advance_down(s)
+        store_scales()

@@ -19,16 +19,23 @@ P = 128
 PACK = 4
 PASS = P * PACK
 PASSES = R // PASS
+N_TILES = N // P
+BANK = 512
 CHUNK = 256
 CHUNKS = T // CHUNK
-HALF = 512
-Y_COLS = 128
-UNITS = [(0, 256, 0), (256, 256, 0), (0, 256, 1), (256, 256, 1), (512, 256, 0), (512, 256, 1), (768, 256, 0), (768, 128, 1), (896, 128, 1)]
-BANK = 512
-LAG = 2
-ADD_LAG = 2
-EARLY_FROM = 768
-VCAST_FROM = 9
+NARROW = 128
+X_LOADS = [(0, 256), (256, 256), (512, 512)]
+WG_LOADS = [(0, 256), (256, 256), (512, 512)]
+STEPS = [(0, 0, 2, 0, 256), (0, 2, 2, 0, 256), (0, 0, 2, 256, 256), (0, 2, 2, 256, 256)] + [(a, i, 1, t, 512) for a, t in ((1, 0), (0, 512), (1, 512)) for i in range(4)]
+CAST_STEP = {(0, 768): 15}
+H_STORES = [(0, 0, 4, 0, 512)] + [(a, i, i + 1, t, t + 512) for a, t in ((1, 0), (0, 512), (1, 512)) for i in range(4)]
+W_STORES = [(0, 0, 1024), (1, 0, 1024)]
+Y_BLOCKS = [(i, 1, t, 512) for t in (0, 512) for i in range(4)]
+Y_STORES = [(i, i + 1, t, t + 512) for t in (0, 512) for i in range(4)]
+CAST_LAG = 2
+ADD_LAG = 1
+V_CASTS = [(1, 256), (1, 768)]
+G_CASTS = []
 
 
 def tile_mix_glusave_gelu_res_kernel(
@@ -37,12 +44,15 @@ def tile_mix_glusave_gelu_res_kernel(
     nc = tc.nc
     with ExitStack() as ctx:
         keep = ctx.enter_context(tc.tile_pool(name="keep", bufs=1))
-        stage = ctx.enter_context(tc.tile_pool(name="stage", bufs=3))
+        stage = ctx.enter_context(tc.tile_pool(name="stage", bufs=4))
         psum = ctx.enter_context(tc.psum_pool(name="psum", bufs=1))
         ctx.enter_context(tc.manual_schedule())
 
         def kept(name, cols, dtype):
             return keep.tile([P, cols], dtype, name=name, align_bytes=64)
+
+        def rows(tile):
+            return tile[:].rearrange("p (i c) -> p i c", i=4)
 
         wu_raw = kept("wu_raw", 2 * R, U8)
         wu_raw_sc = kept("wu_raw_sc", R, U8)
@@ -50,37 +60,33 @@ def tile_mix_glusave_gelu_res_kernel(
         wu_sc = kept("wu_sc", R, U8)
         v4_w = kept("v4_w", PASSES * 2 * N, U8)
         v4_sc = kept("v4_sc", PASSES * N, U8)
-        x_loads = [(0, 1), (1, 1), (2, 2)]
-        x_raw = [kept("x_raw%d" % c, PACK * n * CHUNK, F32) for c, n in x_loads]
+        x_raw = [kept("x_raw%d" % c0, PACK * width, F32) for c0, width in X_LOADS]
+        wg_raw = [kept("wg_raw%d" % c0, PACK * width, F32) for c0, width in WG_LOADS]
         x_bf = [kept("x_bf%d" % c, PACK * CHUNK, BF16) for c in range(CHUNKS)]
-        x_w = [kept("x_w%d" % c, CHUNK, U32) for c in range(CHUNKS)]
-        x_sc = [kept("x_sc%d" % c, CHUNK, U8) for c in range(CHUNKS)]
-        wg_raw = [[kept("wg_raw%d_%d" % (a, b), PACK * 256, F32) for b in range(2)] for a in range(PASSES)]
+        x_w = kept("x_w", T, U32)
+        x_sc = kept("x_sc", T, U8)
         wg_bf = [kept("wg_bf%d" % a, PACK * PASS, BF16) for a in range(PASSES)]
-        wg_w = [[kept("wg_w%d_%d" % (a, q), 256, U32) for q in range(2)] for a in range(PASSES)]
-        wg_sc = [[kept("wg_sc%d_%d" % (a, q), 256, U8) for q in range(2)] for a in range(PASSES)]
-        res_sb = kept("res", 4 * T, F32)
-        y_sb = [kept("y%d" % hf, 4 * HALF, F32) for hf in range(2)]
-        h_sb = [[kept("h%d_%d" % (hf, a), PACK * HALF, F32) for a in range(PASSES)] for hf in range(2)]
-        h_w = [kept("h_w%d" % hf, PASSES * HALF, U32) for hf in range(2)]
+        wg_w = kept("wg_w", R, U32)
+        wg_sc = kept("wg_sc", R, U8)
+        res_sb = kept("res", N_TILES * T, F32)
+        y_sb = kept("y", N_TILES * T, F32)
+        h_sb = [kept("h%d" % a, PACK * T, F32) for a in range(PASSES)]
+        h_w = kept("h_w", PASSES * T, U32)
         h_sc = kept("h_sc", PASSES * T, U8)
 
         nc.vector.memset(wu_raw_sc[:].bitcast(I32), 0)
         nc.vector.memset(v4_sc[:].bitcast(I32), 0)
 
-        def load_x(g):
-            c, n = x_loads[g]
+        def load_columns(tiles, loads, g, src):
+            c0, width = loads[g]
             nc.sync.dma_start(
-                out=x_raw[g][:].rearrange("p (j t) -> p j t", j=PACK),
-                in_=x[:, c * CHUNK : (c + n) * CHUNK].rearrange("(p j) t -> p j t", j=PACK),
+                out=rows(tiles[g]), in_=src[:, c0 : c0 + width].rearrange("(p j) c -> p j c", j=PACK)
             )
 
-        def load_wg(a, b):
-            r0 = a * PASS + b * 256
-            nc.sync.dma_start(
-                out=wg_raw[a][b][:].rearrange("p (j r) -> p j r", j=PACK),
-                in_=wg[:, r0 : r0 + 256].rearrange("(p j) r -> p j r", j=PACK),
-            )
+        def loaded_chunk(tiles, loads, c):
+            for tile, (c0, width) in zip(tiles, loads):
+                if c0 <= c * CHUNK < c0 + width:
+                    return rows(tile)[:, :, c * CHUNK - c0 : (c + 1) * CHUNK - c0]
 
         def load_scales(plane, scales):
             passes = scales.shape[0]
@@ -90,68 +96,66 @@ def tile_mix_glusave_gelu_res_kernel(
                     in_=scales[:, 4 * q : 4 * q + 4, :].rearrange("a r n -> r a n").bitcast(I32),
                 )
 
-        def load_res(hf):
-            nc.sync.dma_start(
-                out=res_sb[:].rearrange("p (i t) -> p i t", i=4),
-                in_=res.rearrange("(i p) t -> p i t", p=P),
-            )
-
         nc.sync.dma_start(out=wu_raw[:].bitcast(I32), in_=wu_words[0].bitcast(I32))
-        load_x(0)
+        load_columns(x_raw, X_LOADS, 0, x)
         load_scales(wu_raw_sc, wu_scales)
-        load_wg(0, 0)
-        load_wg(0, 1)
-        load_x(1)
-        load_wg(1, 0)
-        load_wg(1, 1)
-        load_x(2)
+        for g in range(len(WG_LOADS) - 1):
+            load_columns(wg_raw, WG_LOADS, g, wg)
+        load_columns(x_raw, X_LOADS, 1, x)
+        load_columns(wg_raw, WG_LOADS, 2, wg)
+        load_columns(x_raw, X_LOADS, 2, x)
         load_scales(v4_sc, v4_scales)
         nc.sync.dma_start(
             out=v4_w[:].bitcast(I32).rearrange("p (a n) -> p a n", a=PASSES),
             in_=v4_words.rearrange("a p n -> p a n").bitcast(I32),
         )
-        load_res(0)
+        nc.sync.dma_start(out=rows(res_sb), in_=res.rearrange("(i p) t -> p i t", p=P))
 
         def cast(engine, out, in_):
             if engine == "vector":
                 nc.vector.tensor_copy(out=out, in_=in_)
+            elif engine == "gpsimd":
+                nc.gpsimd.tensor_scalar(out=out, in0=in_, scalar1=1.0, scalar2=0.0, op0=ALU.mult, op1=ALU.add)
             else:
                 nc.scalar.copy(out=out, in_=in_)
 
         def interleave(engine, dst, src):
-            cast(
-                engine,
-                dst.rearrange("p (c i j) -> p c j i", i=4, j=PACK),
-                src.rearrange("p j (c i) -> p c j i", i=4),
-            )
+            if engine == "gpsimd":
+                cast(engine, dst.rearrange("p (c j) -> p c j", j=PACK), src.rearrange("p j c -> p c j"))
+            else:
+                cast(
+                    engine,
+                    dst.rearrange("p (c i j) -> p c j i", i=4, j=PACK),
+                    src.rearrange("p j (c i) -> p c j i", i=4),
+                )
 
         def cast_x(engine, c):
-            interleave(engine, x_bf[c][:], x_raw[min(c, 2)][:].rearrange("p (j t) -> p j t", j=PACK)[:, :, max(c - 2, 0) * CHUNK : (max(c - 2, 0) + 1) * CHUNK])
+            interleave(engine, x_bf[c][:], loaded_chunk(x_raw, X_LOADS, c))
 
         def quantize_x(c):
-            nc.vector.quantize_mx(out=x_w[c][:].bitcast(FP8X4), scales=x_sc[c][:], in_=x_bf[c][:])
+            cols = slice(c * CHUNK, (c + 1) * CHUNK)
+            nc.vector.quantize_mx(out=x_w[:, cols].bitcast(FP8X4), scales=x_sc[:, cols], in_=x_bf[c][:])
 
-        def cast_wg(engine, a, b):
+        def cast_wg(engine, c):
+            a, b = divmod(c, 2)
             dst = wg_bf[a][:].rearrange("p (i m j) -> p m i j", i=PACK, j=PACK)
-            cast(
-                engine,
-                dst[:, 64 * b : 64 * (b + 1), :, :],
-                wg_raw[a][b][:].rearrange("p (j m i) -> p m i j", j=PACK, i=PACK),
-            )
+            src = loaded_chunk(wg_raw, WG_LOADS, c).rearrange("p j (m i) -> p m i j", i=PACK)
+            cast(engine, dst[:, 64 * b : 64 * (b + 1), :, :], src)
 
-        def quantize_wg(a, q):
+        def quantize_wg(c):
+            a, b = divmod(c, 2)
+            cols = slice(c * CHUNK, (c + 1) * CHUNK)
             nc.vector.quantize_mx(
-                out=wg_w[a][q][:].bitcast(FP8X4),
-                scales=wg_sc[a][q][:],
-                in_=wg_bf[a][:, q * 1024 : (q + 1) * 1024],
+                out=wg_w[:, cols].bitcast(FP8X4),
+                scales=wg_sc[:, cols],
+                in_=wg_bf[a][:, b * PACK * CHUNK : (b + 1) * PACK * CHUNK],
             )
 
-        steps = []
-        last_step = []
-        for u, (t0, width, a) in enumerate(UNITS):
-            per_bank = BANK // width
-            steps.extend((u, i0, per_bank) for i0 in range(0, PACK, per_bank))
-            last_step.append(len(steps) - 1)
+        steps = STEPS
+        cast_at = {}
+        for s, (a, i0, count, t0, width) in enumerate(steps):
+            for t in range(t0, t0 + width, CHUNK):
+                cast_at[(a, t)] = s
 
         gate_banks = {}
         up_banks = {}
@@ -159,119 +163,88 @@ def tile_mix_glusave_gelu_res_kernel(
         h_bf = {}
         y_banks = {}
 
-        def x_operand(t0, width):
-            c, w0 = divmod(t0, CHUNK)
-            return x_w[c][:, w0 : w0 + width].bitcast(FP8X4), x_sc[c][:, w0 : w0 + width]
-
-        def gate_matmuls(s):
-            u, i0, count = steps[s]
-            t0, width, a = UNITS[u]
-            rhs, rhs_scale = x_operand(t0, width)
-            bank = psum.tile([P, BANK], F32, name="gate", bufs=3)
-            for e in range(count):
-                q, m0 = divmod((i0 + e) * P, 256)
-                nc.tensor.matmul_mx(
-                    out=bank[:, e * width : (e + 1) * width],
-                    lhsT=wg_w[a][q][:, m0 : m0 + P].bitcast(FP8X4),
-                    lhsT_scale=wg_sc[a][q][:, m0 : m0 + P],
-                    rhs=rhs,
-                    rhs_scale=rhs_scale,
-                    start=True,
-                    stop=True,
-                )
-            gate_banks[s] = bank
-
-        def up_matmuls(s):
-            u, i0, count = steps[s]
-            t0, width, a = UNITS[u]
-            rhs, rhs_scale = x_operand(t0, width)
-            bank = psum.tile([P, BANK], F32, name="up", bufs=3)
+        def hidden_matmuls(s, name, words, scales, bytes_per_word, view):
+            a, i0, count, t0, width = steps[s]
+            bank = psum.tile([P, BANK], F32, name=name, bufs=3 if name == "gate" else 3)
             for e in range(count):
                 m0 = a * PASS + (i0 + e) * P
                 nc.tensor.matmul_mx(
                     out=bank[:, e * width : (e + 1) * width],
-                    lhsT=wu_w[:, 2 * m0 : 2 * (m0 + P)].bitcast(FP4X4),
-                    lhsT_scale=wu_sc[:, m0 : m0 + P],
-                    rhs=rhs,
-                    rhs_scale=rhs_scale,
+                    lhsT=words[:, bytes_per_word * m0 : bytes_per_word * (m0 + P)].bitcast(view),
+                    lhsT_scale=scales[:, m0 : m0 + P],
+                    rhs=x_w[:, t0 : t0 + width].bitcast(FP8X4),
+                    rhs_scale=x_sc[:, t0 : t0 + width],
                     start=True,
                     stop=True,
                 )
-            up_banks[s] = bank
+            return bank
+
+        def gate_matmuls(s):
+            gate_banks[s] = hidden_matmuls(s, "gate", wg_w, wg_sc, 1, FP8X4)
+
+        def up_matmuls(s):
+            up_banks[s] = hidden_matmuls(s, "up", wu_w, wu_sc, 2, FP4X4)
 
         def gelu(s):
-            act = stage.tile([P, BANK], F32, name="act", bufs=4)
+            act = stage.tile([P, BANK], F32, name="act")
             nc.scalar.activation(out=act[:], in_=gate_banks[s][:], func=GELU)
             gelus[s] = act
 
-        def rows_view(tile, t0, width):
-            w0 = t0 % HALF
-            return tile[:].rearrange("p (i t) -> p i t", i=4)[:, :, w0 : w0 + width]
-
         def multiply(s):
-            u, i0, count = steps[s]
-            t0, width, a = UNITS[u]
+            a, i0, count, t0, width = steps[s]
             nc.vector.tensor_tensor(
-                out=rows_view(h_sb[t0 // HALF][a], t0, width)[:, i0 : i0 + count, :],
+                out=rows(h_sb[a])[:, i0 : i0 + count, t0 : t0 + width],
                 in0=up_banks[s][:].rearrange("p (e t) -> p e t", e=count),
                 in1=gelus[s][:].rearrange("p (e t) -> p e t", e=count),
                 op=ALU.mult,
             )
 
-        def cast_h(engine, u):
-            t0, width, a = UNITS[u]
-            rounded = stage.tile([P, PACK * width], BF16, name="rounded", align_bytes=64)
-            interleave(engine, rounded[:], rows_view(h_sb[t0 // HALF][a], t0, width))
-            h_bf[u] = rounded
+        def cast_h(engine, a, t0):
+            rounded = stage.tile([P, PACK * CHUNK], BF16, name="rounded", align_bytes=64)
+            interleave(engine, rounded[:], rows(h_sb[a])[:, :, t0 : t0 + CHUNK])
+            h_bf[(a, t0)] = rounded
 
-        def h_words(a, t0, width):
-            w0 = a * HALF + t0 % HALF
-            return h_w[t0 // HALF][:, w0 : w0 + width]
+        def quantize_h(a, t0):
+            cols = slice(a * T + t0, a * T + t0 + CHUNK)
+            nc.vector.quantize_mx(out=h_w[:, cols].bitcast(FP8X4), scales=h_sc[:, cols], in_=h_bf[(a, t0)][:])
 
-        def h_scales(a, t0, width):
-            return h_sc[:, a * T + t0 : a * T + t0 + width]
+        def down_matmuls(b, name, passes):
+            i0, count, t0, width = Y_BLOCKS[b]
+            bank = y_banks[b] if b in y_banks else psum.tile([P, BANK], F32, name=name, bufs=2 if name == "down" else 3)
+            n_cols = width if width == BANK else NARROW
+            for e in range(count):
+                for t in range(0, width, n_cols):
+                    for a in passes:
+                        n0 = a * N + (i0 + e) * P
+                        cols = slice(a * T + t0 + t, a * T + t0 + t + n_cols)
+                        nc.tensor.matmul_mx(
+                            out=bank[:, e * width + t : e * width + t + n_cols],
+                            lhsT=v4_w[:, 2 * n0 : 2 * (n0 + P)].bitcast(FP4X4),
+                            lhsT_scale=v4_sc[:, n0 : n0 + P],
+                            rhs=h_w[:, cols].bitcast(FP8X4),
+                            rhs_scale=h_sc[:, cols],
+                            start=(a == 0),
+                            stop=(a == PASSES - 1),
+                        )
+            y_banks[b] = bank
 
-        def quantize_h(u):
-            t0, width, a = UNITS[u]
-            nc.vector.quantize_mx(
-                out=h_words(a, t0, width).bitcast(FP8X4), scales=h_scales(a, t0, width), in_=h_bf[u][:]
-            )
-
-        def down_pass(t0, a):
-            if a == 0:
-                y_banks[t0] = psum.tile([P, BANK], F32, name="down", bufs=2)
-            for i in range(4):
-                n0 = a * N + i * P
-                nc.tensor.matmul_mx(
-                    out=y_banks[t0][:, i * Y_COLS : (i + 1) * Y_COLS],
-                    lhsT=v4_w[:, 2 * n0 : 2 * (n0 + P)].bitcast(FP4X4),
-                    lhsT_scale=v4_sc[:, n0 : n0 + P],
-                    rhs=h_words(a, t0, Y_COLS).bitcast(FP8X4),
-                    rhs_scale=h_scales(a, t0, Y_COLS),
-                    start=(a == 0 and i == 0),
-                    stop=(a == PASSES - 1 and i == 3),
-                )
-
-        def add_res(t0):
+        def add_res(b):
+            i0, count, t0, width = Y_BLOCKS[b]
             nc.vector.tensor_tensor(
-                out=rows_view(y_sb[t0 // HALF], t0, Y_COLS),
-                in0=y_banks[t0][:].rearrange("p (i t) -> p i t", i=4),
-                in1=res_sb[:].rearrange("p (i t) -> p i t", i=4)[:, :, t0 : t0 + Y_COLS],
+                out=rows(y_sb)[:, i0 : i0 + count, t0 : t0 + width],
+                in0=y_banks[b][:].rearrange("p (e t) -> p e t", e=count),
+                in1=rows(res_sb)[:, i0 : i0 + count, t0 : t0 + width],
                 op=ALU.add,
             )
 
-        def store_h(a, t0, t1):
-            nc.sync.dma_start(
-                out=out_1[a * PASS : (a + 1) * PASS, t0:t1].rearrange("(p i) t -> p i t", i=PACK),
-                in_=rows_view(h_sb[t0 // HALF][a], t0, t1 - t0),
-            )
+        def store_h(a, i0, i1, t0, t1):
+            dst = out_1[a * PASS : (a + 1) * PASS, :].rearrange("(p i) t -> p i t", i=PACK)
+            nc.sync.dma_start(out=dst[:, i0:i1, t0:t1], in_=rows(h_sb[a])[:, i0:i1, t0:t1])
 
-        def store_words(t0, t1):
-            w0 = t0 % HALF
-            src = h_w[t0 // HALF][:].bitcast(I32).rearrange("p (a t) -> p a t", a=PASSES)
+        def store_words(a, t0, t1):
             nc.sync.dma_start(
-                out=out_2[:, :, t0:t1, :].rearrange("a p t i -> p a (t i)").bitcast(I32),
-                in_=src[:, :, w0 : w0 + t1 - t0],
+                out=out_2[a, :, t0:t1, :].rearrange("p t i -> p (t i)").bitcast(I32),
+                in_=h_w[:, a * T + t0 : a * T + t1].bitcast(I32),
             )
 
         def store_scales():
@@ -281,11 +254,9 @@ def tile_mix_glusave_gelu_res_kernel(
                     in_=h_sc[32 * q : 32 * q + 4, :].bitcast(I32).rearrange("p (a t) -> p a t", a=PASSES),
                 )
 
-        def store_y(t0, t1):
-            nc.sync.dma_start(
-                out=out_0[:, t0:t1].rearrange("(i p) t -> p i t", p=P),
-                in_=rows_view(y_sb[t0 // HALF], t0, t1 - t0),
-            )
+        def store_y(i0, i1, t0, t1):
+            dst = out_0.rearrange("(i p) t -> p i t", p=P)
+            nc.sync.dma_start(out=dst[:, i0:i1, t0:t1], in_=rows(y_sb)[:, i0:i1, t0:t1])
 
         nc.vector.tensor_copy(
             out=wu_w[:].rearrange("p (a i m b) -> p a i m b", a=PASSES, i=PACK, b=2),
@@ -299,83 +270,96 @@ def tile_mix_glusave_gelu_res_kernel(
         quantize_x(0)
         up_matmuls(0)
         up_matmuls(1)
-        cast_wg("vector", 0, 0)
-        cast_wg("vector", 0, 1)
+        cast_wg("vector", 0)
+        cast_wg("vector", 1)
         for s in range(2):
-            quantize_wg(0, s)
+            quantize_wg(s)
             gate_matmuls(s)
         cast_x("vector", 1)
         quantize_x(1)
-        gate_matmuls(2)
+        LOOK = 3
+        if LOOK == 3:
+            gate_matmuls(2)
         up_matmuls(2)
 
-        H_STORES = [{512: 0, 768: 512, 1024: 768}, {256: 0, 512: 256, 768: 512, 1024: 768}]
-        W_STORES = {256: 0, 512: 256, 768: 512, 1024: 768}
-        Y_STORES = {256: 0, 512: 256, 768: 512, 896: 768, 1024: 896}
-        before = {0: [lambda: cast_wg("vector", 1, 0)]}
         after = {
-            0: [lambda: cast_wg("vector", 1, 1)],
-            1: [lambda: quantize_wg(1, 0), lambda: quantize_wg(1, 1)],
+            1: [lambda: cast_wg("scalar", 2), lambda: cast_wg("vector", 3), lambda: quantize_wg(2), lambda: quantize_wg(3)],
             2: [lambda: cast_x("vector", 2)],
-            3: [lambda: quantize_x(2)], 4: [lambda: cast_x("vector", 3)],
-            5: [lambda: quantize_x(3)],
+            3: [lambda: cast_x("vector", 3), lambda: quantize_x(2)], 4: [lambda: quantize_x(3)],
         }
-        waiting = []
-        summed = []
-        opened = list(range(0, T, Y_COLS))
-        quantized = set()
-        started = []
+        h_done = set()
+        y_done = set()
+        q_done = set()
+        h_stores = list(H_STORES)
+        w_stores = list(W_STORES)
+        y_stores = list(Y_STORES)
+        to_cast = sorted(cast_at, key=cast_at.get)
+        to_quantize = []
+        to_sum = list(range(len(Y_BLOCKS)))
+        to_add = []
+        later = []
 
-        def advance_down(s):
-            for t0 in list(started):
-                if (1, t0) in quantized:
-                    down_pass(t0, 1)
-                    started.remove(t0)
-                    summed.append((t0, s))
-            while opened and len(started) + len(summed) < 2 and (0, opened[0]) in quantized and (
-                (1, opened[0]) in quantized or opened[0] >= EARLY_FROM
-            ):
-                t0 = opened.pop(0)
-                down_pass(t0, 0)
-                if (1, t0) in quantized:
-                    down_pass(t0, 1)
-                    summed.append((t0, s))
-                else:
-                    started.append(t0)
+        def chunks_of(t0, t1):
+            return range(t0 - t0 % CHUNK, t1, CHUNK)
 
-        for s in range(len(steps) + 6):
-            if s < len(steps):
+        for s in range(len(steps) + 8):
+            tail = s >= len(steps)
+            waiting, later = later, []
+            if not tail:
                 gelu(s)
-            done = [u for u in range(len(UNITS)) if last_step[u] + LAG == s]
-            for u in done:
-                if u < VCAST_FROM:
-                    cast_h("scalar", u)
-            for job in before.get(s, []):
-                job()
-            if s < len(steps):
+                if s + LOOK < len(steps) and LOOK == 2:
+                    gate_matmuls(s + LOOK)
+            ready = [k for k in to_cast if k not in V_CASTS and max(cast_at[k] + CAST_LAG, CAST_STEP.get(k, 0)) <= s][:1]
+            for k in ready:
+                cast_h("gpsimd" if k in G_CASTS else "scalar", *k)
+                to_cast.remove(k)
+            if not tail:
                 multiply(s)
-                t0, width, a = UNITS[steps[s][0]]
-                if s in last_step and t0 + width in H_STORES[a]:
-                    store_h(a, H_STORES[a][t0 + width], t0 + width)
+                a, i0, count, t0, width = steps[s]
+                for i in range(i0, i0 + count):
+                    for t in chunks_of(t0, t0 + width):
+                        h_done.add((a, i, t))
+            for k in [k for k in to_cast if k in V_CASTS and max(cast_at[k] + 1, CAST_STEP.get(k, 0)) <= s]:
+                cast_h("vector", *k)
+                to_cast.remove(k)
+                later.append(k)
+            for st in list(h_stores):
+                if all((st[0], i, t) in h_done for i in range(st[1], st[2]) for t in chunks_of(st[3], st[4])):
+                    store_h(*st)
+                    h_stores.remove(st)
             for job in after.get(s, []):
                 job()
             if s + 3 < len(steps):
-                gate_matmuls(s + 3)
+                if LOOK == 3:
+                    gate_matmuls(s + 3)
                 up_matmuls(s + 3)
-            if summed and summed[0][1] + ADD_LAG <= s:
-                t0 = summed.pop(0)[0]
-                add_res(t0)
-                if t0 + Y_COLS in Y_STORES:
-                    store_y(Y_STORES[t0 + Y_COLS], t0 + Y_COLS)
-            for u in range(VCAST_FROM, len(UNITS)):
-                if last_step[u] + 1 == s:
-                    cast_h("vector", u)
-            for u in done:
-                quantize_h(u)
-                t0, width, a = UNITS[u]
-                for t in range(t0, t0 + width, Y_COLS):
-                    quantized.add((a, t))
-                if a == PASSES - 1 and t0 + width in W_STORES:
-                    store_words(W_STORES[t0 + width], t0 + width)
-            advance_down(s)
+            if to_add and to_add[0][1] + ADD_LAG <= s:
+                b = to_add.pop(0)[0]
+                add_res(b)
+                i0, count, t0, width = Y_BLOCKS[b]
+                for i in range(i0, i0 + count):
+                    for t in chunks_of(t0, t0 + width):
+                        y_done.add((i, t))
+                for st in list(y_stores):
+                    if all((i, t) in y_done for i in range(st[0], st[1]) for t in chunks_of(st[2], st[3])):
+                        store_y(*st)
+                        y_stores.remove(st)
+            for k in waiting + ready:
+                quantize_h(*k)
+                q_done.add(k)
+            for st in list(w_stores):
+                if all((st[0], t) in q_done for t in chunks_of(st[1], st[2])):
+                    store_words(*st)
+                    w_stores.remove(st)
+            if s == len(steps) - 1 + 0:
+                for b in to_sum:
+                    down_matmuls(b, "gate" if b % 4 >= 2 else "down", [0])
+            while to_sum and len(to_add) < (2 if not tail else 4):
+                i0, count, t0, width = Y_BLOCKS[to_sum[0]]
+                if not all((a, t) in q_done for a in range(PASSES) for t in chunks_of(t0, t0 + width)):
+                    break
+                b = to_sum.pop(0)
+                down_matmuls(b, "down", [1] if b in y_banks else [0, 1])
+                to_add.append((b, s))
         store_scales()
+        assert not (to_cast or to_sum or to_add or h_stores or w_stores or y_stores)

@@ -28,7 +28,7 @@ X_LOADS = [(0, 256), (256, 256), (512, 512)]
 WG_LOADS = [(0, 256), (256, 256), (512, 512)]
 STEPS = [(0, 0, 2, 0, 256), (0, 2, 2, 0, 256), (0, 0, 2, 256, 256), (0, 2, 2, 256, 256)] + [(a, i, 1, t, 512) for a, t in ((1, 0), (0, 512), (1, 512)) for i in range(4)]
 CAST_STEP = {(0, 768): 15}
-H_STORES = [(0, 0, 4, 0, 512)] + [(a, i, i + 1, t, t + 512) for a, t in ((1, 0), (0, 512), (1, 512)) for i in range(4)]
+H_STORES = [(0, 0, 4, 0, 512)] + [(a, i, i + 2, t, t + 512) for a, t in ((1, 0), (0, 512), (1, 512)) for i in (0, 2)]
 W_STORES = [(0, 0, 1024), (1, 0, 1024)]
 Y_BLOCKS = [(i, 1, t, 512) for t in (0, 512) for i in range(4)]
 Y_STORES = [(i, i + 1, t, t + 512) for t in (0, 512) for i in range(4)]

@@ -20,22 +20,19 @@ PACK = 4
 PASS = P * PACK
 PASSES = R // PASS
 N_TILES = N // P
+QUADRANT = 32
+SCALE_ROWS = PASS // 32
 BANK = 512
+HALF = T // 2
 CHUNK = 256
-CHUNKS = T // CHUNK
-NARROW = 128
-X_LOADS = [(0, 256), (256, 256), (512, 512)]
-WG_LOADS = [(0, 256), (256, 256), (512, 512)]
-STEPS = [(0, 0, 2, 0, 256), (0, 2, 2, 0, 256), (0, 0, 2, 256, 256), (0, 2, 2, 256, 256)] + [(a, i, 1, t, 512) for a, t in ((1, 0), (0, 512), (1, 512)) for i in range(4)]
-CAST_STEP = {(0, 768): 15}
-H_STORES = [(0, 0, 4, 0, 512)] + [(a, i, i + 2, t, t + 512) for a, t in ((1, 0), (0, 512), (1, 512)) for i in (0, 2)]
-W_STORES = [(0, 0, 1024), (1, 0, 1024)]
-Y_BLOCKS = [(i, 1, t, 512) for t in (0, 512) for i in range(4)]
-Y_STORES = [(i, i + 1, t, t + 512) for t in (0, 512) for i in range(4)]
-CAST_LAG = 2
-ADD_LAG = 1
-V_CASTS = [(1, 256), (1, 768)]
-G_CASTS = []
+RUN = 4
+
+LOADS = [(0, CHUNK), (CHUNK, CHUNK), (HALF, HALF)]
+
+AHEAD = 3
+Y_BANKS = 2
+STAGE_BUFS = 4
+ROUND_LAG = 2
 
 
 def tile_mix_glusave_gelu_res_kernel(
@@ -44,7 +41,7 @@ def tile_mix_glusave_gelu_res_kernel(
     nc = tc.nc
     with ExitStack() as ctx:
         keep = ctx.enter_context(tc.tile_pool(name="keep", bufs=1))
-        stage = ctx.enter_context(tc.tile_pool(name="stage", bufs=4))
+        stage = ctx.enter_context(tc.tile_pool(name="stage", bufs=STAGE_BUFS))
         psum = ctx.enter_context(tc.psum_pool(name="psum", bufs=1))
         ctx.enter_context(tc.manual_schedule())
 
@@ -60,9 +57,9 @@ def tile_mix_glusave_gelu_res_kernel(
         wu_sc = kept("wu_sc", R, U8)
         v4_w = kept("v4_w", PASSES * 2 * N, U8)
         v4_sc = kept("v4_sc", PASSES * N, U8)
-        x_raw = [kept("x_raw%d" % c0, PACK * width, F32) for c0, width in X_LOADS]
-        wg_raw = [kept("wg_raw%d" % c0, PACK * width, F32) for c0, width in WG_LOADS]
-        x_bf = [kept("x_bf%d" % c, PACK * CHUNK, BF16) for c in range(CHUNKS)]
+        x_raw = [kept("x_raw%d" % c0, PACK * width, F32) for c0, width in LOADS]
+        wg_raw = [kept("wg_raw%d" % c0, PACK * width, F32) for c0, width in LOADS]
+        x_bf = [kept("x_bf%d" % c, PACK * CHUNK, BF16) for c in range(T // CHUNK)]
         x_w = kept("x_w", T, U32)
         x_sc = kept("x_sc", T, U8)
         wg_bf = [kept("wg_bf%d" % a, PACK * PASS, BF16) for a in range(PASSES)]
@@ -77,85 +74,80 @@ def tile_mix_glusave_gelu_res_kernel(
         nc.vector.memset(wu_raw_sc[:].bitcast(I32), 0)
         nc.vector.memset(v4_sc[:].bitcast(I32), 0)
 
-        def load_columns(tiles, loads, g, src):
-            c0, width = loads[g]
+        def load_columns(tiles, g, src):
+            c0, width = LOADS[g]
             nc.sync.dma_start(
                 out=rows(tiles[g]), in_=src[:, c0 : c0 + width].rearrange("(p j) c -> p j c", j=PACK)
             )
 
-        def loaded_chunk(tiles, loads, c):
-            for tile, (c0, width) in zip(tiles, loads):
-                if c0 <= c * CHUNK < c0 + width:
-                    return rows(tile)[:, :, c * CHUNK - c0 : (c + 1) * CHUNK - c0]
+        def loaded_chunk(tiles, c):
+            g = min(c, len(LOADS) - 1)
+            c0 = c * CHUNK - LOADS[g][0]
+            return rows(tiles[g])[:, :, c0 : c0 + CHUNK]
+
+        def plane_rows(plane, q):
+            return plane[q:P:QUADRANT, :].bitcast(I32)
+
+        def scale_rows(scales, q):
+            return scales[:, q:SCALE_ROWS:4, :].rearrange("a r n -> r a n").bitcast(I32)
 
         def load_scales(plane, scales):
-            passes = scales.shape[0]
             for q in range(4):
                 nc.sync.dma_start(
-                    out=plane[32 * q : 32 * q + 4, :].bitcast(I32).rearrange("p (a n) -> p a n", a=passes),
-                    in_=scales[:, 4 * q : 4 * q + 4, :].rearrange("a r n -> r a n").bitcast(I32),
+                    out=plane_rows(plane, q).rearrange("p (a n) -> p a n", a=scales.shape[0]),
+                    in_=scale_rows(scales, q),
                 )
 
         nc.sync.dma_start(out=wu_raw[:].bitcast(I32), in_=wu_words[0].bitcast(I32))
-        load_columns(x_raw, X_LOADS, 0, x)
+        load_columns(x_raw, 0, x)
         load_scales(wu_raw_sc, wu_scales)
-        for g in range(len(WG_LOADS) - 1):
-            load_columns(wg_raw, WG_LOADS, g, wg)
-        load_columns(x_raw, X_LOADS, 1, x)
-        load_columns(wg_raw, WG_LOADS, 2, wg)
-        load_columns(x_raw, X_LOADS, 2, x)
+        load_columns(wg_raw, 0, wg)
+        load_columns(wg_raw, 1, wg)
+        load_columns(x_raw, 1, x)
+        load_columns(wg_raw, 2, wg)
+        load_columns(x_raw, 2, x)
         load_scales(v4_sc, v4_scales)
         nc.sync.dma_start(
             out=v4_w[:].bitcast(I32).rearrange("p (a n) -> p a n", a=PASSES),
             in_=v4_words.rearrange("a p n -> p a n").bitcast(I32),
         )
-        nc.sync.dma_start(out=rows(res_sb), in_=res.rearrange("(i p) t -> p i t", p=P))
+        nc.sync.dma_start(out=rows(res_sb), in_=res.rearrange("(n p) t -> p n t", p=P))
 
-        def cast(engine, out, in_):
-            if engine == "vector":
-                nc.vector.tensor_copy(out=out, in_=in_)
-            elif engine == "gpsimd":
-                nc.gpsimd.tensor_scalar(out=out, in0=in_, scalar1=1.0, scalar2=0.0, op0=ALU.mult, op1=ALU.add)
-            else:
-                nc.scalar.copy(out=out, in_=in_)
+        on_vector = nc.vector.tensor_copy
+        on_scalar = nc.scalar.copy
 
-        def interleave(engine, dst, src):
-            if engine == "gpsimd":
-                cast(engine, dst.rearrange("p (c j) -> p c j", j=PACK), src.rearrange("p j c -> p c j"))
-            else:
-                cast(
-                    engine,
-                    dst.rearrange("p (c i j) -> p c j i", i=4, j=PACK),
-                    src.rearrange("p j (c i) -> p c j i", i=4),
-                )
+        def interleave(copy, dst, src):
+            copy(
+                out=dst.rearrange("p (c e j) -> p c j e", e=RUN, j=PACK),
+                in_=src.rearrange("p j (c e) -> p c j e", e=RUN),
+            )
 
-        def cast_x(engine, c):
-            interleave(engine, x_bf[c][:], loaded_chunk(x_raw, X_LOADS, c))
+        def quantize(words, plane, cols, src):
+            nc.vector.quantize_mx(out=words[:, cols].bitcast(FP8X4), scales=plane[:, cols], in_=src)
+
+        def round_x(copy, c):
+            interleave(copy, x_bf[c][:], loaded_chunk(x_raw, c))
 
         def quantize_x(c):
-            cols = slice(c * CHUNK, (c + 1) * CHUNK)
-            nc.vector.quantize_mx(out=x_w[:, cols].bitcast(FP8X4), scales=x_sc[:, cols], in_=x_bf[c][:])
+            quantize(x_w, x_sc, slice(c * CHUNK, (c + 1) * CHUNK), x_bf[c][:])
 
-        def cast_wg(engine, c):
+        def round_wg(copy, c):
             a, b = divmod(c, 2)
+            per_slot = CHUNK // PACK
             dst = wg_bf[a][:].rearrange("p (i m j) -> p m i j", i=PACK, j=PACK)
-            src = loaded_chunk(wg_raw, WG_LOADS, c).rearrange("p j (m i) -> p m i j", i=PACK)
-            cast(engine, dst[:, 64 * b : 64 * (b + 1), :, :], src)
+            copy(
+                out=dst[:, per_slot * b : per_slot * (b + 1), :, :],
+                in_=loaded_chunk(wg_raw, c).rearrange("p j (m i) -> p m i j", i=PACK),
+            )
 
         def quantize_wg(c):
             a, b = divmod(c, 2)
-            cols = slice(c * CHUNK, (c + 1) * CHUNK)
-            nc.vector.quantize_mx(
-                out=wg_w[:, cols].bitcast(FP8X4),
-                scales=wg_sc[:, cols],
-                in_=wg_bf[a][:, b * PACK * CHUNK : (b + 1) * PACK * CHUNK],
-            )
+            src = wg_bf[a][:, b * PACK * CHUNK : (b + 1) * PACK * CHUNK]
+            quantize(wg_w, wg_sc, slice(c * CHUNK, (c + 1) * CHUNK), src)
 
-        steps = STEPS
-        cast_at = {}
-        for s, (a, i0, count, t0, width) in enumerate(steps):
-            for t in range(t0, t0 + width, CHUNK):
-                cast_at[(a, t)] = s
+        steps = [(0, i0, 2, t0, CHUNK) for t0 in (0, CHUNK) for i0 in (0, 2)]
+        steps.extend((a, i, 1, t0, HALF) for a, t0 in ((1, 0), (0, HALF), (1, HALF)) for i in range(PACK))
+        last_step = len(steps) - 1
 
         gate_banks = {}
         up_banks = {}
@@ -163,15 +155,15 @@ def tile_mix_glusave_gelu_res_kernel(
         h_bf = {}
         y_banks = {}
 
-        def hidden_matmuls(s, name, words, scales, bytes_per_word, view):
+        def hidden_matmuls(s, name, words, plane, elements_per_word, view):
             a, i0, count, t0, width = steps[s]
-            bank = psum.tile([P, BANK], F32, name=name, bufs=3 if name == "gate" else 3)
+            bank = psum.tile([P, BANK], F32, name=name, bufs=AHEAD)
             for e in range(count):
                 m0 = a * PASS + (i0 + e) * P
                 nc.tensor.matmul_mx(
                     out=bank[:, e * width : (e + 1) * width],
-                    lhsT=words[:, bytes_per_word * m0 : bytes_per_word * (m0 + P)].bitcast(view),
-                    lhsT_scale=scales[:, m0 : m0 + P],
+                    lhsT=words[:, elements_per_word * m0 : elements_per_word * (m0 + P)].bitcast(view),
+                    lhsT_scale=plane[:, m0 : m0 + P],
                     rhs=x_w[:, t0 : t0 + width].bitcast(FP8X4),
                     rhs_scale=x_sc[:, t0 : t0 + width],
                     start=True,
@@ -199,167 +191,150 @@ def tile_mix_glusave_gelu_res_kernel(
                 op=ALU.mult,
             )
 
-        def cast_h(engine, a, t0):
+        def round_h(copy, a, t0):
             rounded = stage.tile([P, PACK * CHUNK], BF16, name="rounded", align_bytes=64)
-            interleave(engine, rounded[:], rows(h_sb[a])[:, :, t0 : t0 + CHUNK])
+            interleave(copy, rounded[:], rows(h_sb[a])[:, :, t0 : t0 + CHUNK])
             h_bf[(a, t0)] = rounded
 
         def quantize_h(a, t0):
-            cols = slice(a * T + t0, a * T + t0 + CHUNK)
-            nc.vector.quantize_mx(out=h_w[:, cols].bitcast(FP8X4), scales=h_sc[:, cols], in_=h_bf[(a, t0)][:])
+            quantize(h_w, h_sc, slice(a * T + t0, a * T + t0 + CHUNK), h_bf[(a, t0)][:])
 
-        def down_matmuls(b, name, passes):
-            i0, count, t0, width = Y_BLOCKS[b]
-            bank = y_banks[b] if b in y_banks else psum.tile([P, BANK], F32, name=name, bufs=2 if name == "down" else 3)
-            n_cols = width if width == BANK else NARROW
-            for e in range(count):
-                for t in range(0, width, n_cols):
-                    for a in passes:
-                        n0 = a * N + (i0 + e) * P
-                        cols = slice(a * T + t0 + t, a * T + t0 + t + n_cols)
-                        nc.tensor.matmul_mx(
-                            out=bank[:, e * width + t : e * width + t + n_cols],
-                            lhsT=v4_w[:, 2 * n0 : 2 * (n0 + P)].bitcast(FP4X4),
-                            lhsT_scale=v4_sc[:, n0 : n0 + P],
-                            rhs=h_w[:, cols].bitcast(FP8X4),
-                            rhs_scale=h_sc[:, cols],
-                            start=(a == 0),
-                            stop=(a == PASSES - 1),
-                        )
-            y_banks[b] = bank
-
-        def add_res(b):
-            i0, count, t0, width = Y_BLOCKS[b]
-            nc.vector.tensor_tensor(
-                out=rows(y_sb)[:, i0 : i0 + count, t0 : t0 + width],
-                in0=y_banks[b][:].rearrange("p (e t) -> p e t", e=count),
-                in1=rows(res_sb)[:, i0 : i0 + count, t0 : t0 + width],
-                op=ALU.add,
+        def down_pass(n, t0, a):
+            n0 = a * N + n * P
+            cols = slice(a * T + t0, a * T + t0 + HALF)
+            nc.tensor.matmul_mx(
+                out=y_banks[(n, t0)][:],
+                lhsT=v4_w[:, 2 * n0 : 2 * (n0 + P)].bitcast(FP4X4),
+                lhsT_scale=v4_sc[:, n0 : n0 + P],
+                rhs=h_w[:, cols].bitcast(FP8X4),
+                rhs_scale=h_sc[:, cols],
+                start=(a == 0),
+                stop=(a == PASSES - 1),
             )
 
-        def store_h(a, i0, i1, t0, t1):
-            dst = out_1[a * PASS : (a + 1) * PASS, :].rearrange("(p i) t -> p i t", i=PACK)
-            nc.sync.dma_start(out=dst[:, i0:i1, t0:t1], in_=rows(h_sb[a])[:, i0:i1, t0:t1])
+        def down_first_half(n):
+            y_banks[(n, 0)] = psum.tile([P, BANK], F32, name="down", bufs=Y_BANKS)
+            for a in range(PASSES):
+                down_pass(n, 0, a)
 
-        def store_words(a, t0, t1):
+        def add_and_store_y(n, t0):
+            cols = slice(t0, t0 + HALF)
+            nc.vector.tensor_tensor(
+                out=rows(y_sb)[:, n, cols], in0=y_banks[(n, t0)][:], in1=rows(res_sb)[:, n, cols], op=ALU.add
+            )
+            nc.sync.dma_start(out=out_0[n * P : (n + 1) * P, cols], in_=rows(y_sb)[:, n, cols])
+
+        def store_h(a, i0, i1, t0):
+            dst = out_1[a * PASS : (a + 1) * PASS, :].rearrange("(p i) t -> p i t", i=PACK)
+            nc.sync.dma_start(out=dst[:, i0:i1, t0 : t0 + HALF], in_=rows(h_sb[a])[:, i0:i1, t0 : t0 + HALF])
+
+        def store_words(a):
             nc.sync.dma_start(
-                out=out_2[a, :, t0:t1, :].rearrange("p t i -> p (t i)").bitcast(I32),
-                in_=h_w[:, a * T + t0 : a * T + t1].bitcast(I32),
+                out=out_2[a].rearrange("p t i -> p (t i)").bitcast(I32),
+                in_=h_w[:, a * T : (a + 1) * T].bitcast(I32),
             )
 
         def store_scales():
             for q in range(4):
                 nc.sync.dma_start(
-                    out=out_3[:, 4 * q : 4 * q + 4, :].rearrange("a r t -> r a t").bitcast(I32),
-                    in_=h_sc[32 * q : 32 * q + 4, :].bitcast(I32).rearrange("p (a t) -> p a t", a=PASSES),
+                    out=scale_rows(out_3, q), in_=plane_rows(h_sc, q).rearrange("p (a t) -> p a t", a=PASSES)
                 )
-
-        def store_y(i0, i1, t0, t1):
-            dst = out_0.rearrange("(i p) t -> p i t", p=P)
-            nc.sync.dma_start(out=dst[:, i0:i1, t0:t1], in_=rows(y_sb)[:, i0:i1, t0:t1])
 
         nc.vector.tensor_copy(
             out=wu_w[:].rearrange("p (a i m b) -> p a i m b", a=PASSES, i=PACK, b=2),
             in_=wu_raw[:].rearrange("p (a m i b) -> p a i m b", a=PASSES, i=PACK, b=2),
         )
-        cast_x("scalar", 0)
+        round_x(on_scalar, 0)
         nc.vector.tensor_copy(
             out=wu_sc[:].rearrange("p (a i m) -> p a i m", a=PASSES, i=PACK),
             in_=wu_raw_sc[:].rearrange("p (a m i) -> p a i m", a=PASSES, i=PACK),
         )
+
         quantize_x(0)
         up_matmuls(0)
         up_matmuls(1)
-        cast_wg("vector", 0)
-        cast_wg("vector", 1)
+        round_wg(on_vector, 0)
+        round_wg(on_vector, 1)
         for s in range(2):
             quantize_wg(s)
             gate_matmuls(s)
-        cast_x("vector", 1)
+        round_x(on_vector, 1)
         quantize_x(1)
-        LOOK = 3
-        if LOOK == 3:
-            gate_matmuls(2)
+        gate_matmuls(2)
         up_matmuls(2)
 
-        after = {
-            1: [lambda: cast_wg("scalar", 2), lambda: cast_wg("vector", 3), lambda: quantize_wg(2), lambda: quantize_wg(3)],
-            2: [lambda: cast_x("vector", 2)],
-            3: [lambda: cast_x("vector", 3), lambda: quantize_x(2)], 4: [lambda: quantize_x(3)],
-        }
-        h_done = set()
-        y_done = set()
-        q_done = set()
-        h_stores = list(H_STORES)
-        w_stores = list(W_STORES)
-        y_stores = list(Y_STORES)
-        to_cast = sorted(cast_at, key=cast_at.get)
-        to_quantize = []
-        to_sum = list(range(len(Y_BLOCKS)))
-        to_add = []
-        later = []
+        def prepare_operands(s):
+            if s == 1:
+                round_wg(on_scalar, 2)
+                round_wg(on_vector, 3)
+                quantize_wg(2)
+                quantize_wg(3)
+            if s in (2, 3):
+                round_x(on_vector, s)
+            if s in (3, 4):
+                quantize_x(s - 1)
 
-        def chunks_of(t0, t1):
-            return range(t0 - t0 % CHUNK, t1, CHUNK)
+        multiplied = {}
+        for s, (a, i0, count, t0, width) in enumerate(steps):
+            for t in range(t0, t0 + width, CHUNK):
+                multiplied[(a, t)] = s
+        vector_rounds = {multiplied[key] + 1: key for key in [(1, CHUNK), (1, HALF + CHUNK)]}
+        scalar_rounds = {}
+        for key, s in multiplied.items():
+            if vector_rounds.get(s + 1) != key:
+                due = s + ROUND_LAG
+                scalar_rounds[due + 2 if due in scalar_rounds else due] = key
+        first_half_ready = multiplied[(1, 0)] + ROUND_LAG
+        second_half_ready = multiplied[(1, HALF)] + ROUND_LAG
 
-        for s in range(len(steps) + 8):
-            tail = s >= len(steps)
-            waiting, later = later, []
-            if not tail:
+        for s in range(second_half_ready + 1):
+            if s <= last_step:
                 gelu(s)
-                if s + LOOK < len(steps) and LOOK == 2:
-                    gate_matmuls(s + LOOK)
-            ready = [k for k in to_cast if k not in V_CASTS and max(cast_at[k] + CAST_LAG, CAST_STEP.get(k, 0)) <= s][:1]
-            for k in ready:
-                cast_h("gpsimd" if k in G_CASTS else "scalar", *k)
-                to_cast.remove(k)
-            if not tail:
+            if s in scalar_rounds:
+                round_h(on_scalar, *scalar_rounds[s])
+            if s <= last_step:
                 multiply(s)
-                a, i0, count, t0, width = steps[s]
-                for i in range(i0, i0 + count):
-                    for t in chunks_of(t0, t0 + width):
-                        h_done.add((a, i, t))
-            for k in [k for k in to_cast if k in V_CASTS and max(cast_at[k] + 1, CAST_STEP.get(k, 0)) <= s]:
-                cast_h("vector", *k)
-                to_cast.remove(k)
-                later.append(k)
-            for st in list(h_stores):
-                if all((st[0], i, t) in h_done for i in range(st[1], st[2]) for t in chunks_of(st[3], st[4])):
-                    store_h(*st)
-                    h_stores.remove(st)
-            for job in after.get(s, []):
-                job()
-            if s + 3 < len(steps):
-                if LOOK == 3:
-                    gate_matmuls(s + 3)
-                up_matmuls(s + 3)
-            if to_add and to_add[0][1] + ADD_LAG <= s:
-                b = to_add.pop(0)[0]
-                add_res(b)
-                i0, count, t0, width = Y_BLOCKS[b]
-                for i in range(i0, i0 + count):
-                    for t in chunks_of(t0, t0 + width):
-                        y_done.add((i, t))
-                for st in list(y_stores):
-                    if all((i, t) in y_done for i in range(st[0], st[1]) for t in chunks_of(st[2], st[3])):
-                        store_y(*st)
-                        y_stores.remove(st)
-            for k in waiting + ready:
-                quantize_h(*k)
-                q_done.add(k)
-            for st in list(w_stores):
-                if all((st[0], t) in q_done for t in chunks_of(st[1], st[2])):
-                    store_words(*st)
-                    w_stores.remove(st)
-            if s == len(steps) - 1 + 0:
-                for b in to_sum:
-                    down_matmuls(b, "gate" if b % 4 >= 2 else "down", [0])
-            while to_sum and len(to_add) < (2 if not tail else 4):
-                i0, count, t0, width = Y_BLOCKS[to_sum[0]]
-                if not all((a, t) in q_done for a in range(PASSES) for t in chunks_of(t0, t0 + width)):
-                    break
-                b = to_sum.pop(0)
-                down_matmuls(b, "down", [1] if b in y_banks else [0, 1])
-                to_add.append((b, s))
+            if s in vector_rounds:
+                round_h(on_vector, *vector_rounds[s])
+
+            if s == 3:
+                store_h(0, 0, PACK, 0)
+            elif 3 < s <= last_step and s % 2 == 1:
+                a, i, count, t0, width = steps[s]
+                store_h(a, i - 1, i + 1, t0)
+
+            prepare_operands(s)
+            if s + AHEAD <= last_step:
+                gate_matmuls(s + AHEAD)
+                up_matmuls(s + AHEAD)
+
+            n = s - first_half_ready - 1
+            if 0 <= n < N_TILES:
+                add_and_store_y(n, 0)
+
+            if s - 1 in vector_rounds:
+                quantize_h(*vector_rounds[s - 1])
+            if s in scalar_rounds:
+                quantize_h(*scalar_rounds[s])
+
+            if s == first_half_ready:
+                for first in range(Y_BANKS):
+                    down_first_half(first)
+            elif 0 <= n < N_TILES - Y_BANKS:
+                down_first_half(n + Y_BANKS)
+
+            if s == last_step:
+                store_words(0)
+                for n in range(N_TILES):
+                    if n < Y_BANKS:
+                        y_banks[(n, HALF)] = psum.tile([P, BANK], F32, name="down", bufs=Y_BANKS)
+                    else:
+                        y_banks[(n, HALF)] = psum.tile([P, BANK], F32, name="gate", bufs=AHEAD)
+                    down_pass(n, HALF, 0)
+
+        store_words(1)
         store_scales()
-        assert not (to_cast or to_sum or to_add or h_stores or w_stores or y_stores)
+        for n in range(N_TILES):
+            down_pass(n, HALF, 1)
+        for n in range(N_TILES):
+            add_and_store_y(n, HALF)

from contextlib import ExitStack

import concourse.mybir as mybir

K, R, N, T = 512, 1024, 512, 1024
FLOPS = 2 * K * R * T * 2 + 2 * R * N * T

F32 = mybir.dt.float32
BF16 = mybir.dt.bfloat16
I32 = mybir.dt.int32
U32 = mybir.dt.uint32
U8 = mybir.dt.uint8
FP8X4 = mybir.dt.float8_e4m3fn_x4
FP4X4 = mybir.dt.float4_e2m1fn_x4
ALU = mybir.AluOpType
GELU = mybir.ActivationFunctionType.Gelu_apprx_tanh

P = 128
PACK = 4
PASS = P * PACK
PASSES = R // PASS
N_TILES = N // P
QUADRANT = 32
SCALE_ROWS = PASS // 32
BANK = 512
HALF = T // 2
CHUNK = 256
RUN = 4

LOADS = [(0, CHUNK), (CHUNK, CHUNK), (HALF, HALF)]

AHEAD = 3
Y_BANKS = 2
STAGE_BUFS = 4
ROUND_LAG = 2


def tile_mix_glusave_gelu_res_kernel(
    tc, x, wg, wu_words, wu_scales, v4_words, v4_scales, res, out_0, out_1, out_2, out_3
):
    nc = tc.nc
    with ExitStack() as ctx:
        keep = ctx.enter_context(tc.tile_pool(name="keep", bufs=1))
        stage = ctx.enter_context(tc.tile_pool(name="stage", bufs=STAGE_BUFS))
        psum = ctx.enter_context(tc.psum_pool(name="psum", bufs=1))
        ctx.enter_context(tc.manual_schedule())

        def kept(name, cols, dtype):
            return keep.tile([P, cols], dtype, name=name, align_bytes=64)

        def rows(tile):
            return tile[:].rearrange("p (i c) -> p i c", i=4)

        wu_raw = kept("wu_raw", 2 * R, U8)
        wu_raw_sc = kept("wu_raw_sc", R, U8)
        wu_w = kept("wu_w", 2 * R, U8)
        wu_sc = kept("wu_sc", R, U8)
        v4_w = kept("v4_w", PASSES * 2 * N, U8)
        v4_sc = kept("v4_sc", PASSES * N, U8)
        x_raw = [kept("x_raw%d" % c0, PACK * width, F32) for c0, width in LOADS]
        wg_raw = [kept("wg_raw%d" % c0, PACK * width, F32) for c0, width in LOADS]
        x_bf = [kept("x_bf%d" % c, PACK * CHUNK, BF16) for c in range(T // CHUNK)]
        x_w = kept("x_w", T, U32)
        x_sc = kept("x_sc", T, U8)
        wg_bf = [kept("wg_bf%d" % a, PACK * PASS, BF16) for a in range(PASSES)]
        wg_w = kept("wg_w", R, U32)
        wg_sc = kept("wg_sc", R, U8)
        res_sb = kept("res", N_TILES * T, F32)
        y_sb = kept("y", N_TILES * T, F32)
        h_sb = [kept("h%d" % a, PACK * T, F32) for a in range(PASSES)]
        h_w = kept("h_w", PASSES * T, U32)
        h_sc = kept("h_sc", PASSES * T, U8)

        nc.vector.memset(wu_raw_sc[:].bitcast(I32), 0)
        nc.vector.memset(v4_sc[:].bitcast(I32), 0)

        def load_columns(tiles, g, src):
            c0, width = LOADS[g]
            nc.sync.dma_start(
                out=rows(tiles[g]), in_=src[:, c0 : c0 + width].rearrange("(p j) c -> p j c", j=PACK)
            )

        def loaded_chunk(tiles, c):
            g = min(c, len(LOADS) - 1)
            c0 = c * CHUNK - LOADS[g][0]
            return rows(tiles[g])[:, :, c0 : c0 + CHUNK]

        def plane_rows(plane, q):
            return plane[q:P:QUADRANT, :].bitcast(I32)

        def scale_rows(scales, q):
            return scales[:, q:SCALE_ROWS:4, :].rearrange("a r n -> r a n").bitcast(I32)

        def load_scales(plane, scales):
            for q in range(4):
                nc.sync.dma_start(
                    out=plane_rows(plane, q).rearrange("p (a n) -> p a n", a=scales.shape[0]),
                    in_=scale_rows(scales, q),
                )

        nc.sync.dma_start(out=wu_raw[:].bitcast(I32), in_=wu_words[0].bitcast(I32))
        load_columns(x_raw, 0, x)
        load_scales(wu_raw_sc, wu_scales)
        load_columns(wg_raw, 0, wg)
        load_columns(wg_raw, 1, wg)
        load_columns(x_raw, 1, x)
        load_columns(wg_raw, 2, wg)
        load_columns(x_raw, 2, x)
        load_scales(v4_sc, v4_scales)
        nc.sync.dma_start(
            out=v4_w[:].bitcast(I32).rearrange("p (a n) -> p a n", a=PASSES),
            in_=v4_words.rearrange("a p n -> p a n").bitcast(I32),
        )
        nc.sync.dma_start(out=rows(res_sb), in_=res.rearrange("(n p) t -> p n t", p=P))

        on_vector = nc.vector.tensor_copy
        on_scalar = nc.scalar.copy

        def interleave(copy, dst, src):
            copy(
                out=dst.rearrange("p (c e j) -> p c j e", e=RUN, j=PACK),
                in_=src.rearrange("p j (c e) -> p c j e", e=RUN),
            )

        def quantize(words, plane, cols, src):
            nc.vector.quantize_mx(out=words[:, cols].bitcast(FP8X4), scales=plane[:, cols], in_=src)

        def round_x(copy, c):
            interleave(copy, x_bf[c][:], loaded_chunk(x_raw, c))

        def quantize_x(c):
            quantize(x_w, x_sc, slice(c * CHUNK, (c + 1) * CHUNK), x_bf[c][:])

        def round_wg(copy, c):
            a, b = divmod(c, 2)
            per_slot = CHUNK // PACK
            dst = wg_bf[a][:].rearrange("p (i m j) -> p m i j", i=PACK, j=PACK)
            copy(
                out=dst[:, per_slot * b : per_slot * (b + 1), :, :],
                in_=loaded_chunk(wg_raw, c).rearrange("p j (m i) -> p m i j", i=PACK),
            )

        def quantize_wg(c):
            a, b = divmod(c, 2)
            src = wg_bf[a][:, b * PACK * CHUNK : (b + 1) * PACK * CHUNK]
            quantize(wg_w, wg_sc, slice(c * CHUNK, (c + 1) * CHUNK), src)

        steps = [(0, i0, 2, t0, CHUNK) for t0 in (0, CHUNK) for i0 in (0, 2)]
        steps.extend((a, i, 1, t0, HALF) for a, t0 in ((1, 0), (0, HALF), (1, HALF)) for i in range(PACK))
        last_step = len(steps) - 1

        gate_banks = {}
        up_banks = {}
        gelus = {}
        h_bf = {}
        y_banks = {}

        def hidden_matmuls(s, name, words, plane, elements_per_word, view):
            a, i0, count, t0, width = steps[s]
            bank = psum.tile([P, BANK], F32, name=name, bufs=AHEAD)
            for e in range(count):
                m0 = a * PASS + (i0 + e) * P
                nc.tensor.matmul_mx(
                    out=bank[:, e * width : (e + 1) * width],
                    lhsT=words[:, elements_per_word * m0 : elements_per_word * (m0 + P)].bitcast(view),
                    lhsT_scale=plane[:, m0 : m0 + P],
                    rhs=x_w[:, t0 : t0 + width].bitcast(FP8X4),
                    rhs_scale=x_sc[:, t0 : t0 + width],
                    start=True,
                    stop=True,
                )
            return bank

        def gate_matmuls(s):
            gate_banks[s] = hidden_matmuls(s, "gate", wg_w, wg_sc, 1, FP8X4)

        def up_matmuls(s):
            up_banks[s] = hidden_matmuls(s, "up", wu_w, wu_sc, 2, FP4X4)

        def gelu(s):
            act = stage.tile([P, BANK], F32, name="act")
            nc.scalar.activation(out=act[:], in_=gate_banks[s][:], func=GELU)
            gelus[s] = act

        def multiply(s):
            a, i0, count, t0, width = steps[s]
            nc.vector.tensor_tensor(
                out=rows(h_sb[a])[:, i0 : i0 + count, t0 : t0 + width],
                in0=up_banks[s][:].rearrange("p (e t) -> p e t", e=count),
                in1=gelus[s][:].rearrange("p (e t) -> p e t", e=count),
                op=ALU.mult,
            )

        def round_h(copy, a, t0):
            rounded = stage.tile([P, PACK * CHUNK], BF16, name="rounded", align_bytes=64)
            interleave(copy, rounded[:], rows(h_sb[a])[:, :, t0 : t0 + CHUNK])
            h_bf[(a, t0)] = rounded

        def quantize_h(a, t0):
            quantize(h_w, h_sc, slice(a * T + t0, a * T + t0 + CHUNK), h_bf[(a, t0)][:])

        def down_pass(n, t0, a):
            n0 = a * N + n * P
            cols = slice(a * T + t0, a * T + t0 + HALF)
            nc.tensor.matmul_mx(
                out=y_banks[(n, t0)][:],
                lhsT=v4_w[:, 2 * n0 : 2 * (n0 + P)].bitcast(FP4X4),
                lhsT_scale=v4_sc[:, n0 : n0 + P],
                rhs=h_w[:, cols].bitcast(FP8X4),
                rhs_scale=h_sc[:, cols],
                start=(a == 0),
                stop=(a == PASSES - 1),
            )

        def down_first_half(n):
            y_banks[(n, 0)] = psum.tile([P, BANK], F32, name="down", bufs=Y_BANKS)
            for a in range(PASSES):
                down_pass(n, 0, a)

        def add_and_store_y(n, t0):
            cols = slice(t0, t0 + HALF)
            nc.vector.tensor_tensor(
                out=rows(y_sb)[:, n, cols], in0=y_banks[(n, t0)][:], in1=rows(res_sb)[:, n, cols], op=ALU.add
            )
            nc.sync.dma_start(out=out_0[n * P : (n + 1) * P, cols], in_=rows(y_sb)[:, n, cols])

        def store_h(a, i0, i1, t0):
            dst = out_1[a * PASS : (a + 1) * PASS, :].rearrange("(p i) t -> p i t", i=PACK)
            nc.sync.dma_start(out=dst[:, i0:i1, t0 : t0 + HALF], in_=rows(h_sb[a])[:, i0:i1, t0 : t0 + HALF])

        def store_words(a):
            nc.sync.dma_start(
                out=out_2[a].rearrange("p t i -> p (t i)").bitcast(I32),
                in_=h_w[:, a * T : (a + 1) * T].bitcast(I32),
            )

        def store_scales():
            for q in range(4):
                nc.sync.dma_start(
                    out=scale_rows(out_3, q), in_=plane_rows(h_sc, q).rearrange("p (a t) -> p a t", a=PASSES)
                )

        nc.vector.tensor_copy(
            out=wu_w[:].rearrange("p (a i m b) -> p a i m b", a=PASSES, i=PACK, b=2),
            in_=wu_raw[:].rearrange("p (a m i b) -> p a i m b", a=PASSES, i=PACK, b=2),
        )
        round_x(on_scalar, 0)
        nc.vector.tensor_copy(
            out=wu_sc[:].rearrange("p (a i m) -> p a i m", a=PASSES, i=PACK),
            in_=wu_raw_sc[:].rearrange("p (a m i) -> p a i m", a=PASSES, i=PACK),
        )

        quantize_x(0)
        up_matmuls(0)
        up_matmuls(1)
        round_wg(on_vector, 0)
        round_wg(on_vector, 1)
        for s in range(2):
            quantize_wg(s)
            gate_matmuls(s)
        round_x(on_vector, 1)
        quantize_x(1)
        gate_matmuls(2)
        up_matmuls(2)

        def prepare_operands(s):
            if s == 1:
                round_wg(on_scalar, 2)
                round_wg(on_vector, 3)
                quantize_wg(2)
                quantize_wg(3)
            if s in (2, 3):
                round_x(on_vector, s)
            if s in (3, 4):
                quantize_x(s - 1)

        multiplied = {}
        for s, (a, i0, count, t0, width) in enumerate(steps):
            for t in range(t0, t0 + width, CHUNK):
                multiplied[(a, t)] = s
        vector_rounds = {multiplied[key] + 1: key for key in [(1, CHUNK), (1, HALF + CHUNK)]}
        scalar_rounds = {}
        for key, s in multiplied.items():
            if vector_rounds.get(s + 1) != key:
                due = s + ROUND_LAG
                scalar_rounds[due + 2 if due in scalar_rounds else due] = key
        first_half_ready = multiplied[(1, 0)] + ROUND_LAG
        second_half_ready = multiplied[(1, HALF)] + ROUND_LAG

        for s in range(second_half_ready + 1):
            if s <= last_step:
                gelu(s)
            if s in scalar_rounds:
                round_h(on_scalar, *scalar_rounds[s])
            if s <= last_step:
                multiply(s)
            if s in vector_rounds:
                round_h(on_vector, *vector_rounds[s])

            if s == 3:
                store_h(0, 0, PACK, 0)
            elif 3 < s <= last_step and s % 2 == 1:
                a, i, count, t0, width = steps[s]
                store_h(a, i - 1, i + 1, t0)

            prepare_operands(s)
            if s + AHEAD <= last_step:
                gate_matmuls(s + AHEAD)
                up_matmuls(s + AHEAD)

            n = s - first_half_ready - 1
            if 0 <= n < N_TILES:
                add_and_store_y(n, 0)

            if s - 1 in vector_rounds:
                quantize_h(*vector_rounds[s - 1])
            if s in scalar_rounds:
                quantize_h(*scalar_rounds[s])

            if s == first_half_ready:
                for first in range(Y_BANKS):
                    down_first_half(first)
            elif 0 <= n < N_TILES - Y_BANKS:
                down_first_half(n + Y_BANKS)

            if s == last_step:
                store_words(0)
                for n in range(N_TILES):
                    if n < Y_BANKS:
                        y_banks[(n, HALF)] = psum.tile([P, BANK], F32, name="down", bufs=Y_BANKS)
                    else:
                        y_banks[(n, HALF)] = psum.tile([P, BANK], F32, name="gate", bufs=AHEAD)
                    down_pass(n, HALF, 0)

        store_words(1)
        store_scales()
        for n in range(N_TILES):
            down_pass(n, HALF, 1)
        for n in range(N_TILES):
            add_and_store_y(n, HALF)
